import numpy as np
import ml_dtypes


def mxq(x, axis, fmt="e4m3"):
    dtype, down = {"e4m3": (ml_dtypes.float8_e4m3fn, 7), "e5m2": (ml_dtypes.float8_e5m2, 14)}[fmt]
    v = np.moveaxis(np.asarray(x, np.float32).astype(ml_dtypes.bfloat16).astype(np.float64), axis, -1)
    blocks = v.reshape(v.shape[:-1] + (-1, 32))
    amax = np.abs(blocks).max(-1, keepdims=True)
    byte = np.maximum(np.where(amax > 0, np.frexp(amax)[1] - 1 + 127, 0) - down, 1)
    scale = np.exp2(byte - 127.0)
    codes = (blocks / scale).astype(np.float32).astype(dtype).astype(np.float64)
    return np.moveaxis((codes * scale).reshape(v.shape), -1, axis)


WIDE = False


def mx_kscale(k):
    if not WIDE:
        return np.ones(k)
    levels = np.array([10, -10, 5, -5, 0])
    if k % 512:
        return np.exp2(np.random.permutation(np.resize(levels, k // 32))).repeat(32)
    a = np.empty((k // 512, 16))
    for p in range(k // 512):
        a[p, :8] = np.random.permutation(np.resize(levels, 8))
        for g in range(8):
            far = levels[np.abs(levels - a[p, g]) >= 10]
            a[p, g + 8] = far[np.random.randint(len(far))]
    return np.exp2(a.ravel()).repeat(32)


def f64(x):
    return np.asarray(x).astype(np.float64)


def striped(idx):
    return np.tile(np.asarray(idx).reshape(-1, 16).T, (8, 1)).astype(np.uint16)


def unstriped(offs):
    return offs[:16].T.reshape(-1).astype(np.int64)


E2M1 = np.array([0.0, 0.5, 1.0, 1.5, 2.0, 3.0, 4.0, 6.0, -0.0, -0.5, -1.0, -1.5, -2.0, -3.0, -4.0, -6.0])


def pack_weight(w, fmt):
    k, n = w.shape
    w = f64(np.asarray(w, np.float32).astype(ml_dtypes.bfloat16)).reshape(k // 32, 32, n)
    amax = np.abs(w).max(1)
    if fmt == "e4m3":
        byte = np.frexp(amax)[1] - 1 + 127 - 7
    else:
        mant, ex = np.frexp(amax / 6.0)
        byte = np.where(mant > 0.5, ex, ex - 1) + 127
    byte = np.clip(np.where(amax > 0, byte, 1), 1, 254)
    scaled = (w * np.exp2(127.0 - byte)[:, None, :]).reshape(k, n).astype(np.float32)
    by_word = np.ascontiguousarray(scaled.reshape(k // 512, 128, 4, n).transpose(0, 1, 3, 2))
    if fmt == "e4m3":
        words = by_word.astype(ml_dtypes.float8_e4m3fn).view(np.uint8)
    else:
        c = by_word.astype(ml_dtypes.float4_e2m1fn).view(np.uint8) & 0xF
        words = (c[..., 0::2] | (c[..., 1::2] << 4)).reshape(k // 512, 128, 2 * n)
    return np.ascontiguousarray(words), np.ascontiguousarray(byte.astype(np.uint8).reshape(k // 512, 16, n))


def unpack_weight(words, scales, fmt):
    g, _, n = scales.shape
    words = np.ascontiguousarray(words).reshape(g, 128, n, -1)
    if fmt == "e4m3":
        vals = words.view(ml_dtypes.float8_e4m3fn).astype(np.float64)
    else:
        nib = np.empty((g, 128, n, 4), np.uint8)
        nib[..., 0::2] = words & 0xF
        nib[..., 1::2] = words >> 4
        vals = E2M1[nib]
    vals = vals * np.repeat(np.exp2(scales.astype(np.float64) - 127.0), 8, axis=1)[..., None]
    return vals.transpose(0, 1, 3, 2).reshape(g * 512, n)


B, N, T, D, NQ = 1, 512, 2048, 512, 256


def setup_inputs():
    n = np.random.standard_normal
    idx = np.random.permutation(T)[:B * N]
    s = mx_kscale(D)[:, None]
    kp = pack_weight(n((D, T)) / s, "e4m3")
    return {
        "qT": (n((B, D, NQ)) * s * (1.00 / np.sqrt(D))).astype(np.float32),
        "k_words": kp[0],
        "k_scales": kp[1],
        "rk": np.tile(np.random.uniform(0.5, 1.0, 2048), (128, 1)).astype(np.float32),
        "rq": (np.random.uniform(0.05, 0.15, (B, NQ, 1))).astype(np.float32),
        "offs": striped(idx),
    }


def reference(qT, k_words, k_scales, rk, rq, offs):
    idx = unstriped(offs)
    pick = lambda x, which: x[:, which].reshape(x.shape[0], B, -1).transpose(1, 0, 2)
    k = unpack_weight(k_words, k_scales, "e4m3")
    kg = pick(k, idx)
    qq = mxq(f64(qT), 1, "e4m3")
    a = qq.transpose(0, 2, 1) @ kg
    y = np.exp(10.0 * a * pick(f64(rk), idx)[:, :1, :] * f64(rq) - 10.0)
    return y

@@ -1,0 +1,124 @@
+from contextlib import ExitStack
+
+import concourse.mybir as mybir
+from concourse.masks import make_identity
+
+D, NQ, N, T = 512, 256, 512, 2048
+FLOPS = 2 * D * NQ * N
+
+F32 = mybir.dt.float32
+BF16 = mybir.dt.bfloat16
+I32 = mybir.dt.int32
+U32 = mybir.dt.uint32
+U16 = mybir.dt.uint16
+U8 = mybir.dt.uint8
+FP8X4 = mybir.dt.float8_e4m3fn_x4
+EXP = mybir.ActivationFunctionType.Exp
+MULT = mybir.AluOpType.mult
+
+P = 128
+PACK = 4
+QT = NQ // P
+HALVES = 2
+NH = N // HALVES
+BLOCKS = NH // P
+RK_PART = 4
+
+
+def tile_attend_cosexp_topk_kernel(tc, qT, k_words, k_scales, rk, rq, offs, out):
+    nc = tc.nc
+    with ExitStack() as ctx:
+        keep = ctx.enter_context(tc.tile_pool(name="keep", bufs=1))
+        psum = ctx.enter_context(tc.psum_pool(name="psum", bufs=1))
+
+        offsets = keep.tile([P, N // 16], U16, name="offsets")
+        nc.sync.dma_start(offsets[:], offs)
+
+        q_raw = keep.tile([P, PACK, NQ], F32, name="q_raw")
+        nc.scalar.dma_start(q_raw[:], qT[0].rearrange("(p j) n -> p j n", j=PACK))
+        word_pool = keep.tile([P, T], I32, name="word_pool", align_bytes=64)
+        nc.scalar.dma_start(word_pool[:], k_words[0].rearrange("p t r -> p (t r)").bitcast(I32))
+
+        minus_ten = keep.tile([P, 1], F32, name="minus_ten")
+        nc.gpsimd.memset(minus_ten[:], -10.0)
+        warm = keep.tile([P, 1], F32, name="warm")
+        nc.scalar.activation(warm[:], minus_ten[:], EXP, bias=minus_ten[:], scale=1.0)
+
+        rk_pool = keep.tile([P, T], F32, name="rk_pool", align_bytes=64)
+        nc.vector.memset(rk_pool[:], 0.0)
+        nc.sync.dma_start(rk_pool[RK_PART : RK_PART + 1, :], rk[0:1, :])
+
+        scale_pool = keep.tile([P, T // 4], I32, name="scale_pool", tag="slot_a", align_bytes=64)
+        nc.vector.memset(scale_pool[:], 0)
+        for quad in range(4):
+            nc.sync.dma_start(
+                scale_pool[32 * quad : 32 * quad + 4, :],
+                k_scales[0, 4 * quad : 4 * quad + 4, :].bitcast(I32),
+            )
+
+        rq_sb = keep.tile([P, QT], F32, name="rq_sb")
+        nc.sync.dma_start(rq_sb[:], rq[0].rearrange("(p m) o -> p (m o)", m=QT))
+
+        ident = keep.tile([P, P], F32, name="ident")
+        nc.vector.memset(ident[:], 0.0)
+        make_identity(nc, ident[:], nomemset=True)
+
+        q_by_tile = q_raw[:].rearrange("p j (n m) -> p m n j", m=QT)
+        q_bf = keep.tile([P, QT, P, PACK], BF16, name="q_bf", tag="slot_b", align_bytes=64)
+        for m in range(QT):
+            nc.scalar.copy(q_bf[:, m], q_by_tile[:, m])
+
+        half_offsets = [offsets[:, h * NH // 16 : (h + 1) * NH // 16] for h in range(HALVES)]
+
+        rk_all = []
+        for h in range(HALVES):
+            rk_row = keep.tile([P, NH], F32, name="rk_row%d" % h, align_bytes=64)
+            nc.vector.tensor_copy(rk_row[:], rk_pool[:].indirect(half_offsets[h]))
+            turned = psum.tile([P, BLOCKS, P], F32, name="turned%d" % h)
+            for b in range(BLOCKS):
+                nc.tensor.transpose(turned[:, b, :], rk_row[:, b * P : (b + 1) * P], ident[:])
+            rk_col = keep.tile([P, BLOCKS], F32, name="rk_col%d" % h)
+            nc.scalar.copy(rk_col[:], turned[:, :, RK_PART])
+            spread = psum.tile([P, BLOCKS, P], F32, name="spread%d" % h)
+            for b in range(BLOCKS):
+                nc.tensor.transpose(spread[:, b, :], rk_col[:, b : b + 1].to_broadcast([P, P]), ident[:])
+            rk_half = keep.tile([P, NH], F32, name="rk_half%d" % h)
+            nc.scalar.copy(rk_half[:], spread[:].rearrange("p b n -> p (b n)"))
+            rk_all.append(rk_half)
+
+        k_scale = keep.tile([P, N], U8, name="k_scale", align_bytes=64)
+        nc.vector.tensor_copy(k_scale[:], scale_pool[:].bitcast(U8).indirect(offsets[:]))
+
+        q_codes = keep.tile([P, NQ], U32, name="q_codes", tag="slot_a", align_bytes=64)
+        q_scale = keep.tile([P, NQ], U8, name="q_scale", align_bytes=64)
+        nc.vector.quantize_mx(
+            out=q_codes[:].bitcast(FP8X4),
+            scales=q_scale[:],
+            in_=q_bf[:].rearrange("p m n j -> p (m n j)"),
+        )
+
+        k_codes = keep.tile([P, N], U32, name="k_codes", tag="slot_b", align_bytes=64)
+        for h in range(HALVES):
+            slots = slice(h * NH, (h + 1) * NH)
+            nc.vector.tensor_copy(k_codes[:, slots], word_pool[:].bitcast(U32).indirect(half_offsets[h]))
+
+        out_by_tile = out[0].rearrange("(p m) n -> p m n", m=QT)
+        for h in range(HALVES):
+            slots = slice(h * NH, (h + 1) * NH)
+            for m in range(QT):
+                rows = slice(m * P, (m + 1) * P)
+                acc = psum.tile([P, NH], F32, name="acc%d%d" % (h, m))
+                nc.tensor.matmul_mx(
+                    out=acc[:],
+                    lhsT=q_codes[:, rows].bitcast(FP8X4),
+                    lhsT_scale=q_scale[:, rows],
+                    rhs=k_codes[:, slots].bitcast(FP8X4),
+                    rhs_scale=k_scale[:, slots],
+                    start=True,
+                    stop=True,
+                )
+                scaled = keep.tile([P, NH], F32, name="scaled%d%d" % (h, m))
+                nc.vector.scalar_tensor_tensor(scaled[:], acc[:], 10.0, rk_all[h][:], MULT, MULT)
+                res = keep.tile([P, NH], F32, name="res%d%d" % (h, m))
+                nc.scalar.activation(res[:], scaled[:], EXP, bias=minus_ten[:], scale=rq_sb[:, m : m + 1])
+                nc.sync.dma_start(out_by_tile[:, m, slots], res[:])

@@ -34,41 +34,46 @@ def tile_attend_cosexp_topk_kernel(tc, qT, k_words, k_scales, rk, rq, offs, out)
         offsets = keep.tile([P, N // 16], U16, name="offsets")
         nc.sync.dma_start(offsets[:], offs)
 
-        q_raw = keep.tile([P, PACK, NQ], F32, name="q_raw")
-        nc.scalar.dma_start(q_raw[:], qT[0].rearrange("(p j) n -> p j n", j=PACK))
-        word_pool = keep.tile([P, T], I32, name="word_pool", align_bytes=64)
-        nc.scalar.dma_start(word_pool[:], k_words[0].rearrange("p t r -> p (t r)").bitcast(I32))
+        rq_sb = keep.tile([P, QT], F32, name="rq_sb")
+        nc.sync.dma_start(rq_sb[:], rq[0].rearrange("(p m) o -> p (m o)", m=QT))
 
-        minus_ten = keep.tile([P, 1], F32, name="minus_ten")
-        nc.gpsimd.memset(minus_ten[:], -10.0)
-        warm = keep.tile([P, 1], F32, name="warm")
-        nc.scalar.activation(warm[:], minus_ten[:], EXP, bias=minus_ten[:], scale=1.0)
-
-        rk_pool = keep.tile([P, T], F32, name="rk_pool", align_bytes=64)
-        nc.vector.memset(rk_pool[:], 0.0)
-        nc.sync.dma_start(rk_pool[RK_PART : RK_PART + 1, :], rk[0:1, :])
-
-        scale_pool = keep.tile([P, T // 4], I32, name="scale_pool", tag="slot_a", align_bytes=64)
+        scale_pool = keep.tile([P, T // 4], I32, name="scale_pool", align_bytes=64)
         nc.vector.memset(scale_pool[:], 0)
         for quad in range(4):
-            nc.sync.dma_start(
+            queue = nc.sync if quad < 2 else nc.scalar
+            queue.dma_start(
                 scale_pool[32 * quad : 32 * quad + 4, :],
                 k_scales[0, 4 * quad : 4 * quad + 4, :].bitcast(I32),
             )
 
-        rq_sb = keep.tile([P, QT], F32, name="rq_sb")
-        nc.sync.dma_start(rq_sb[:], rq[0].rearrange("(p m) o -> p (m o)", m=QT))
+        minus_ten = keep.tile([P, 1], F32, name="minus_ten")
+        nc.vector.memset(minus_ten[:], -10.0)
+        warm = keep.tile([P, 1], F32, name="warm")
+        nc.scalar.activation(warm[:], minus_ten[:], EXP, bias=minus_ten[:], scale=1.0)
+
+        q_raw = keep.tile([P, PACK, NQ], F32, name="q_raw")
+        nc.sync.dma_start(q_raw[:], qT[0].rearrange("(p j) n -> p j n", j=PACK))
+
+        rk_pool = keep.tile([P, T], F32, name="rk_pool", tag="slot_a", align_bytes=64)
+        nc.vector.memset(rk_pool[:], 0.0)
+        nc.sync.dma_start(rk_pool[RK_PART : RK_PART + 1, :], rk[0:1, :])
+
+        word_pool = keep.tile([P, T], I32, name="word_pool", align_bytes=64)
+        nc.sync.dma_start(word_pool[:], k_words[0].rearrange("p t r -> p (t r)").bitcast(I32))
 
         ident = keep.tile([P, P], F32, name="ident")
         nc.vector.memset(ident[:], 0.0)
         make_identity(nc, ident[:], nomemset=True)
 
         q_by_tile = q_raw[:].rearrange("p j (n m) -> p m n j", m=QT)
-        q_bf = keep.tile([P, QT, P, PACK], BF16, name="q_bf", tag="slot_b", align_bytes=64)
+        q_bf = keep.tile([P, QT, P, PACK], BF16, name="q_bf", align_bytes=64)
         for m in range(QT):
             nc.scalar.copy(q_bf[:, m], q_by_tile[:, m])
 
         half_offsets = [offsets[:, h * NH // 16 : (h + 1) * NH // 16] for h in range(HALVES)]
+
+        k_scale = keep.tile([P, N], U8, name="k_scale", align_bytes=64)
+        nc.vector.tensor_copy(k_scale[:], scale_pool[:].bitcast(U8).indirect(offsets[:]))
 
         rk_all = []
         for h in range(HALVES):
@@ -86,9 +91,6 @@ def tile_attend_cosexp_topk_kernel(tc, qT, k_words, k_scales, rk, rq, offs, out)
             nc.scalar.copy(rk_half[:], spread[:].rearrange("p b n -> p (b n)"))
             rk_all.append(rk_half)
 
-        k_scale = keep.tile([P, N], U8, name="k_scale", align_bytes=64)
-        nc.vector.tensor_copy(k_scale[:], scale_pool[:].bitcast(U8).indirect(offsets[:]))
-
         q_codes = keep.tile([P, NQ], U32, name="q_codes", tag="slot_a", align_bytes=64)
         q_scale = keep.tile([P, NQ], U8, name="q_scale", align_bytes=64)
         nc.vector.quantize_mx(
@@ -97,7 +99,7 @@ def tile_attend_cosexp_topk_kernel(tc, qT, k_words, k_scales, rk, rq, offs, out)
             in_=q_bf[:].rearrange("p m n j -> p (m n j)"),
         )
 
-        k_codes = keep.tile([P, N], U32, name="k_codes", tag="slot_b", align_bytes=64)
+        k_codes = keep.tile([P, N], U32, name="k_codes", align_bytes=64)
         for h in range(HALVES):
             slots = slice(h * NH, (h + 1) * NH)
             nc.vector.tensor_copy(k_codes[:, slots], word_pool[:].bitcast(U32).indirect(half_offsets[h]))

@@ -14,6 +14,7 @@ U16 = mybir.dt.uint16
 U8 = mybir.dt.uint8
 FP8X4 = mybir.dt.float8_e4m3fn_x4
 EXP = mybir.ActivationFunctionType.Exp
+COPY = mybir.ActivationFunctionType.Copy
 MULT = mybir.AluOpType.mult
 
 P = 128
@@ -34,25 +35,24 @@ def tile_attend_cosexp_topk_kernel(tc, qT, k_words, k_scales, rk, rq, offs, out)
         offsets = keep.tile([P, N // 16], U16, name="offsets")
         nc.sync.dma_start(offsets[:], offs)
 
+        rq_raw = keep.tile([P, QT], F32, name="rq_raw")
+        nc.scalar.dma_start(rq_raw[:], rq[0].rearrange("(p m) o -> p (m o)", m=QT))
         rq_sb = keep.tile([P, QT], F32, name="rq_sb")
-        nc.sync.dma_start(rq_sb[:], rq[0].rearrange("(p m) o -> p (m o)", m=QT))
+        nc.scalar.activation(rq_sb[:], rq_raw[:], COPY, scale=10.0)
+
+        q_rows = qT[0].rearrange("(p j) n -> p j n", j=PACK)
+        q_raw = keep.tile([P, PACK, NQ], F32, name="q_raw")
+        nc.sync.dma_start(q_raw[:, : PACK // 2], q_rows[:, : PACK // 2])
 
         scale_pool = keep.tile([P, T // 4], I32, name="scale_pool", align_bytes=64)
         nc.vector.memset(scale_pool[:], 0)
         for quad in range(4):
-            queue = nc.sync if quad < 2 else nc.scalar
-            queue.dma_start(
+            nc.sync.dma_start(
                 scale_pool[32 * quad : 32 * quad + 4, :],
                 k_scales[0, 4 * quad : 4 * quad + 4, :].bitcast(I32),
             )
 
-        minus_ten = keep.tile([P, 1], F32, name="minus_ten")
-        nc.vector.memset(minus_ten[:], -10.0)
-        warm = keep.tile([P, 1], F32, name="warm")
-        nc.scalar.activation(warm[:], minus_ten[:], EXP, bias=minus_ten[:], scale=1.0)
-
-        q_raw = keep.tile([P, PACK, NQ], F32, name="q_raw")
-        nc.sync.dma_start(q_raw[:], qT[0].rearrange("(p j) n -> p j n", j=PACK))
+        nc.sync.dma_start(q_raw[:, PACK // 2 :], q_rows[:, PACK // 2 :])
 
         rk_pool = keep.tile([P, T], F32, name="rk_pool", tag="slot_a", align_bytes=64)
         nc.vector.memset(rk_pool[:], 0.0)
@@ -61,6 +61,9 @@ def tile_attend_cosexp_topk_kernel(tc, qT, k_words, k_scales, rk, rq, offs, out)
         word_pool = keep.tile([P, T], I32, name="word_pool", align_bytes=64)
         nc.sync.dma_start(word_pool[:], k_words[0].rearrange("p t r -> p (t r)").bitcast(I32))
 
+        minus_ten = keep.tile([P, 1], F32, name="minus_ten")
+        nc.vector.memset(minus_ten[:], -10.0)
+
         ident = keep.tile([P, P], F32, name="ident")
         nc.vector.memset(ident[:], 0.0)
         make_identity(nc, ident[:], nomemset=True)
@@ -68,7 +71,7 @@ def tile_attend_cosexp_topk_kernel(tc, qT, k_words, k_scales, rk, rq, offs, out)
         q_by_tile = q_raw[:].rearrange("p j (n m) -> p m n j", m=QT)
         q_bf = keep.tile([P, QT, P, PACK], BF16, name="q_bf", align_bytes=64)
         for m in range(QT):
-            nc.scalar.copy(q_bf[:, m], q_by_tile[:, m])
+            nc.scalar.activation(q_bf[:, m], q_by_tile[:, m], COPY)
 
         half_offsets = [offsets[:, h * NH // 16 : (h + 1) * NH // 16] for h in range(HALVES)]
 
@@ -119,8 +122,12 @@ def tile_attend_cosexp_topk_kernel(tc, qT, k_words, k_scales, rk, rq, offs, out)
                     start=True,
                     stop=True,
                 )
-                scaled = keep.tile([P, NH], F32, name="scaled%d%d" % (h, m))
-                nc.vector.scalar_tensor_tensor(scaled[:], acc[:], 10.0, rk_all[h][:], MULT, MULT)
-                res = keep.tile([P, NH], F32, name="res%d%d" % (h, m))
-                nc.scalar.activation(res[:], scaled[:], EXP, bias=minus_ten[:], scale=rq_sb[:, m : m + 1])
-                nc.sync.dma_start(out_by_tile[:, m, slots], res[:])
+                last = h == HALVES - 1 and m == QT - 1
+                width = NH // 2 if last else NH
+                for c0 in range(0, NH, width):
+                    cols = slice(c0, c0 + width)
+                    scaled = keep.tile([P, width], F32, name="scaled%d%d%d" % (h, m, c0))
+                    nc.vector.tensor_tensor(scaled[:], acc[:, cols], rk_all[h][:, cols], MULT)
+                    res = keep.tile([P, width], F32, name="res%d%d%d" % (h, m, c0))
+                    nc.scalar.activation(res[:], scaled[:], EXP, bias=minus_ten[:], scale=rq_sb[:, m : m + 1])
+                    nc.sync.dma_start(out_by_tile[:, m, h * NH + c0 : h * NH + c0 + width], res[:])

@@ -1,7 +1,6 @@
 from contextlib import ExitStack
 
 import concourse.mybir as mybir
-from concourse.masks import make_identity
 
 D, NQ, N, T = 512, 256, 512, 2048
 FLOPS = 2 * D * NQ * N
@@ -40,11 +39,14 @@ def tile_attend_cosexp_topk_kernel(tc, qT, k_words, k_scales, rk, rq, offs, out)
         rq_sb = keep.tile([P, QT], F32, name="rq_sb")
         nc.scalar.activation(rq_sb[:], rq_raw[:], COPY, scale=10.0)
 
-        q_rows = qT[0].rearrange("(p j) n -> p j n", j=PACK)
         q_raw = keep.tile([P, PACK, NQ], F32, name="q_raw")
-        nc.sync.dma_start(q_raw[:, : PACK // 2], q_rows[:, : PACK // 2])
+        nc.sync.dma_start(q_raw[:], qT[0].rearrange("(p j) n -> p j n", j=PACK))
 
-        scale_pool = keep.tile([P, T // 4], I32, name="scale_pool", align_bytes=64)
+        rk_pool = keep.tile([P, T], F32, name="rk_pool", align_bytes=64)
+        nc.vector.memset(rk_pool[:], 0.0)
+        nc.sync.dma_start(rk_pool[RK_PART : RK_PART + 1, :], rk[0:1, :])
+
+        scale_pool = keep.tile([P, T // 4], I32, name="scale_pool", tag="slot_a", align_bytes=64)
         nc.vector.memset(scale_pool[:], 0)
         for quad in range(4):
             nc.sync.dma_start(
@@ -52,21 +54,24 @@ def tile_attend_cosexp_topk_kernel(tc, qT, k_words, k_scales, rk, rq, offs, out)
                 k_scales[0, 4 * quad : 4 * quad + 4, :].bitcast(I32),
             )
 
-        nc.sync.dma_start(q_raw[:, PACK // 2 :], q_rows[:, PACK // 2 :])
+        zeros = keep.tile([P, P], F32, name="zeros", tag="slot_b", align_bytes=64)
+        nc.vector.memset(zeros[:], 0.0)
+        ident = keep.tile([P, P], F32, name="ident")
+        nc.gpsimd.affine_select(
+            out=ident[:],
+            in_=zeros[:],
+            compare_op=mybir.AluOpType.not_equal,
+            fill=1.0,
+            base=0,
+            pattern=[[-1, P]],
+            channel_multiplier=1,
+        )
 
-        rk_pool = keep.tile([P, T], F32, name="rk_pool", tag="slot_a", align_bytes=64)
-        nc.vector.memset(rk_pool[:], 0.0)
-        nc.sync.dma_start(rk_pool[RK_PART : RK_PART + 1, :], rk[0:1, :])
-
-        word_pool = keep.tile([P, T], I32, name="word_pool", align_bytes=64)
+        word_pool = keep.tile([P, T], I32, name="word_pool", tag="slot_b", align_bytes=64)
         nc.sync.dma_start(word_pool[:], k_words[0].rearrange("p t r -> p (t r)").bitcast(I32))
 
         minus_ten = keep.tile([P, 1], F32, name="minus_ten")
         nc.vector.memset(minus_ten[:], -10.0)
-
-        ident = keep.tile([P, P], F32, name="ident")
-        nc.vector.memset(ident[:], 0.0)
-        make_identity(nc, ident[:], nomemset=True)
 
         q_by_tile = q_raw[:].rearrange("p j (n m) -> p m n j", m=QT)
         q_bf = keep.tile([P, QT, P, PACK], BF16, name="q_bf", align_bytes=64)
@@ -74,9 +79,6 @@ def tile_attend_cosexp_topk_kernel(tc, qT, k_words, k_scales, rk, rq, offs, out)
             nc.scalar.activation(q_bf[:, m], q_by_tile[:, m], COPY)
 
         half_offsets = [offsets[:, h * NH // 16 : (h + 1) * NH // 16] for h in range(HALVES)]
-
-        k_scale = keep.tile([P, N], U8, name="k_scale", align_bytes=64)
-        nc.vector.tensor_copy(k_scale[:], scale_pool[:].bitcast(U8).indirect(offsets[:]))
 
         rk_all = []
         for h in range(HALVES):
@@ -93,6 +95,9 @@ def tile_attend_cosexp_topk_kernel(tc, qT, k_words, k_scales, rk, rq, offs, out)
             rk_half = keep.tile([P, NH], F32, name="rk_half%d" % h)
             nc.scalar.copy(rk_half[:], spread[:].rearrange("p b n -> p (b n)"))
             rk_all.append(rk_half)
+
+        k_scale = keep.tile([P, N], U8, name="k_scale", align_bytes=64)
+        nc.vector.tensor_copy(k_scale[:], scale_pool[:].bitcast(U8).indirect(offsets[:]))
 
         q_codes = keep.tile([P, NQ], U32, name="q_codes", tag="slot_a", align_bytes=64)
         q_scale = keep.tile([P, NQ], U8, name="q_scale", align_bytes=64)

@@ -1,6 +1,7 @@
 from contextlib import ExitStack
 
 import concourse.mybir as mybir
+from concourse.masks import make_identity
 
 D, NQ, N, T = 512, 256, 512, 2048
 FLOPS = 2 * D * NQ * N
@@ -22,7 +23,7 @@ QT = NQ // P
 HALVES = 2
 NH = N // HALVES
 BLOCKS = NH // P
-RK_PART = 4
+RK_PART = P - 1
 
 
 def tile_attend_cosexp_topk_kernel(tc, qT, k_words, k_scales, rk, rq, offs, out):
@@ -34,67 +35,54 @@ def tile_attend_cosexp_topk_kernel(tc, qT, k_words, k_scales, rk, rq, offs, out)
         offsets = keep.tile([P, N // 16], U16, name="offsets")
         nc.sync.dma_start(offsets[:], offs)
 
-        rq_raw = keep.tile([P, QT], F32, name="rq_raw")
-        nc.scalar.dma_start(rq_raw[:], rq[0].rearrange("(p m) o -> p (m o)", m=QT))
-        rq_sb = keep.tile([P, QT], F32, name="rq_sb")
-        nc.scalar.activation(rq_sb[:], rq_raw[:], COPY, scale=10.0)
-
-        q_raw = keep.tile([P, PACK, NQ], F32, name="q_raw")
-        nc.sync.dma_start(q_raw[:], qT[0].rearrange("(p j) n -> p j n", j=PACK))
-
-        rk_pool = keep.tile([P, T], F32, name="rk_pool", align_bytes=64)
-        nc.vector.memset(rk_pool[:], 0.0)
-        nc.sync.dma_start(rk_pool[RK_PART : RK_PART + 1, :], rk[0:1, :])
-
         scale_pool = keep.tile([P, T // 4], I32, name="scale_pool", tag="slot_a", align_bytes=64)
         nc.vector.memset(scale_pool[:], 0)
+        rk_pool = keep.tile([P, T], F32, name="rk_pool", align_bytes=64)
+        nc.vector.memset(rk_pool[:RK_PART, :], 0.0)
+
+        nc.sync.dma_start(rk_pool[RK_PART : RK_PART + 1, :], rk[0:1, :])
+
+        q_raw = keep.tile([P, PACK, NQ], F32, name="q_raw", tag="slot_b")
+        nc.sync.dma_start(q_raw[:], qT[0].rearrange("(p j) n -> p j n", j=PACK))
+
         for quad in range(4):
             nc.sync.dma_start(
                 scale_pool[32 * quad : 32 * quad + 4, :],
                 k_scales[0, 4 * quad : 4 * quad + 4, :].bitcast(I32),
             )
 
-        zeros = keep.tile([P, P], F32, name="zeros", tag="slot_b", align_bytes=64)
-        nc.vector.memset(zeros[:], 0.0)
-        ident = keep.tile([P, P], F32, name="ident")
-        nc.gpsimd.affine_select(
-            out=ident[:],
-            in_=zeros[:],
-            compare_op=mybir.AluOpType.not_equal,
-            fill=1.0,
-            base=0,
-            pattern=[[-1, P]],
-            channel_multiplier=1,
-        )
-
-        word_pool = keep.tile([P, T], I32, name="word_pool", tag="slot_b", align_bytes=64)
+        word_pool = keep.tile([P, T], I32, name="word_pool", align_bytes=64)
         nc.sync.dma_start(word_pool[:], k_words[0].rearrange("p t r -> p (t r)").bitcast(I32))
 
+        rq_sb = keep.tile([P, QT], F32, name="rq_sb")
+        nc.sync.dma_start(rq_sb[:], rq[0].rearrange("(p m) o -> p (m o)", m=QT))
+
+        ident = keep.tile([P, P], F32, name="ident")
+        make_identity(nc, ident[:])
         minus_ten = keep.tile([P, 1], F32, name="minus_ten")
-        nc.vector.memset(minus_ten[:], -10.0)
+        nc.gpsimd.memset(minus_ten[:], -10.0)
 
         q_by_tile = q_raw[:].rearrange("p j (n m) -> p m n j", m=QT)
-        q_bf = keep.tile([P, QT, P, PACK], BF16, name="q_bf", align_bytes=64)
+        q_bf = keep.tile([P, QT, P, PACK], BF16, name="q_bf", tag="slot_c", align_bytes=64)
         for m in range(QT):
             nc.scalar.activation(q_bf[:, m], q_by_tile[:, m], COPY)
 
         half_offsets = [offsets[:, h * NH // 16 : (h + 1) * NH // 16] for h in range(HALVES)]
 
-        rk_all = []
+        rk_row = keep.tile([P, N], F32, name="rk_row", align_bytes=64)
+        nc.vector.tensor_copy(rk_row[:], rk_pool[:].indirect(offsets[:]))
+        turned = psum.tile([P, N // P, P], F32, name="turned")
+        for b in range(N // P):
+            nc.tensor.transpose(turned[:, b, :], rk_row[:, b * P : (b + 1) * P], ident[:])
+        rk_col = keep.tile([P, N // P], F32, name="rk_col", tag="slot_b")
+        nc.scalar.copy(rk_col[:], turned[:, :, RK_PART])
+        rk_all = keep.tile([P, N], F32, name="rk_all")
         for h in range(HALVES):
-            rk_row = keep.tile([P, NH], F32, name="rk_row%d" % h, align_bytes=64)
-            nc.vector.tensor_copy(rk_row[:], rk_pool[:].indirect(half_offsets[h]))
-            turned = psum.tile([P, BLOCKS, P], F32, name="turned%d" % h)
-            for b in range(BLOCKS):
-                nc.tensor.transpose(turned[:, b, :], rk_row[:, b * P : (b + 1) * P], ident[:])
-            rk_col = keep.tile([P, BLOCKS], F32, name="rk_col%d" % h)
-            nc.scalar.copy(rk_col[:], turned[:, :, RK_PART])
             spread = psum.tile([P, BLOCKS, P], F32, name="spread%d" % h)
             for b in range(BLOCKS):
-                nc.tensor.transpose(spread[:, b, :], rk_col[:, b : b + 1].to_broadcast([P, P]), ident[:])
-            rk_half = keep.tile([P, NH], F32, name="rk_half%d" % h)
-            nc.scalar.copy(rk_half[:], spread[:].rearrange("p b n -> p (b n)"))
-            rk_all.append(rk_half)
+                col = h * BLOCKS + b
+                nc.tensor.transpose(spread[:, b, :], rk_col[:, col : col + 1].to_broadcast([P, P]), ident[:])
+            nc.scalar.activation(rk_all[:, h * NH : (h + 1) * NH], spread[:].rearrange("p b n -> p (b n)"), COPY, scale=10.0)
 
         k_scale = keep.tile([P, N], U8, name="k_scale", align_bytes=64)
         nc.vector.tensor_copy(k_scale[:], scale_pool[:].bitcast(U8).indirect(offsets[:]))
@@ -107,7 +95,7 @@ def tile_attend_cosexp_topk_kernel(tc, qT, k_words, k_scales, rk, rq, offs, out)
             in_=q_bf[:].rearrange("p m n j -> p (m n j)"),
         )
 
-        k_codes = keep.tile([P, N], U32, name="k_codes", align_bytes=64)
+        k_codes = keep.tile([P, N], U32, name="k_codes", tag="slot_c", align_bytes=64)
         for h in range(HALVES):
             slots = slice(h * NH, (h + 1) * NH)
             nc.vector.tensor_copy(k_codes[:, slots], word_pool[:].bitcast(U32).indirect(half_offsets[h]))
@@ -132,7 +120,7 @@ def tile_attend_cosexp_topk_kernel(tc, qT, k_words, k_scales, rk, rq, offs, out)
                 for c0 in range(0, NH, width):
                     cols = slice(c0, c0 + width)
                     scaled = keep.tile([P, width], F32, name="scaled%d%d%d" % (h, m, c0))
-                    nc.vector.tensor_tensor(scaled[:], acc[:, cols], rk_all[h][:, cols], MULT)
+                    nc.vector.tensor_tensor(scaled[:], acc[:, cols], rk_all[:, h * NH + c0 : h * NH + c0 + width], MULT)
                     res = keep.tile([P, width], F32, name="res%d%d%d" % (h, m, c0))
                     nc.scalar.activation(res[:], scaled[:], EXP, bias=minus_ten[:], scale=rq_sb[:, m : m + 1])
                     nc.sync.dma_start(out_by_tile[:, m, h * NH + c0 : h * NH + c0 + width], res[:])

@@ -24,32 +24,31 @@ HALVES = 2
 NH = N // HALVES
 BLOCKS = NH // P
 RK_PART = P - 1
+SCALE_ROWS = D // 32
+SCALE_PART = 64 - SCALE_ROWS
 
 
 def tile_attend_cosexp_topk_kernel(tc, qT, k_words, k_scales, rk, rq, offs, out):
     nc = tc.nc
     with ExitStack() as ctx:
         keep = ctx.enter_context(tc.tile_pool(name="keep", bufs=1))
+        reuse = ctx.enter_context(tc.tile_pool(name="reuse", bufs=1))
         psum = ctx.enter_context(tc.psum_pool(name="psum", bufs=1))
 
         offsets = keep.tile([P, N // 16], U16, name="offsets")
         nc.sync.dma_start(offsets[:], offs)
 
-        scale_pool = keep.tile([P, T // 4], I32, name="scale_pool", tag="slot_a", align_bytes=64)
-        nc.vector.memset(scale_pool[:], 0)
-        rk_pool = keep.tile([P, T], F32, name="rk_pool", align_bytes=64)
-        nc.vector.memset(rk_pool[:RK_PART, :], 0.0)
+        scale_pool = keep.tile([P, T // 4], I32, name="scale_pool", align_bytes=64)
+        nc.vector.memset(scale_pool[:SCALE_PART, :], 0)
+        nc.vector.memset(scale_pool[64:, :], 0)
+        nc.sync.dma_start(scale_pool[SCALE_PART:64, :], k_scales[0].bitcast(I32))
 
-        nc.sync.dma_start(rk_pool[RK_PART : RK_PART + 1, :], rk[0:1, :])
+        rk_pool = reuse.tile([P, T], F32, name="rk_pool", offset=0, align_bytes=64)
+        nc.vector.memset(rk_pool[:RK_PART, :], 0.0)
+        nc.scalar.dma_start(rk_pool[RK_PART : RK_PART + 1, :], rk[0:1, :])
 
         q_raw = keep.tile([P, PACK, NQ], F32, name="q_raw", tag="slot_b")
         nc.sync.dma_start(q_raw[:], qT[0].rearrange("(p j) n -> p j n", j=PACK))
-
-        for quad in range(4):
-            nc.sync.dma_start(
-                scale_pool[32 * quad : 32 * quad + 4, :],
-                k_scales[0, 4 * quad : 4 * quad + 4, :].bitcast(I32),
-            )
 
         word_pool = keep.tile([P, T], I32, name="word_pool", align_bytes=64)
         nc.sync.dma_start(word_pool[:], k_words[0].rearrange("p t r -> p (t r)").bitcast(I32))
@@ -57,37 +56,45 @@ def tile_attend_cosexp_topk_kernel(tc, qT, k_words, k_scales, rk, rq, offs, out)
         rq_sb = keep.tile([P, QT], F32, name="rq_sb")
         nc.sync.dma_start(rq_sb[:], rq[0].rearrange("(p m) o -> p (m o)", m=QT))
 
+        k_zero = keep.tile([P, 1], F32, name="k_zero")
+        nc.gpsimd.memset(k_zero[:], 0.0)
+        k_scale = keep.tile([P, N // 4], I32, name="k_scale", align_bytes=64)
+        nc.gpsimd.memset(k_scale[:], 0)
         ident = keep.tile([P, P], F32, name="ident")
         make_identity(nc, ident[:])
         minus_ten = keep.tile([P, 1], F32, name="minus_ten")
-        nc.gpsimd.memset(minus_ten[:], -10.0)
+        nc.scalar.activation(minus_ten[:], k_zero[:], COPY, bias=-10.0)
+
+        picked_scales = keep.tile([P, N], U8, name="picked_scales", align_bytes=64)
+        nc.vector.tensor_copy(picked_scales[:], scale_pool[:].bitcast(U8).indirect(offsets[:]))
+        for quad in range(4):
+            first = SCALE_PART + 4 * quad
+            nc.sync.dma_start(k_scale[32 * quad : 32 * quad + 4, :], picked_scales[first : first + 4, :].bitcast(I32))
 
         q_by_tile = q_raw[:].rearrange("p j (n m) -> p m n j", m=QT)
-        q_bf = keep.tile([P, QT, P, PACK], BF16, name="q_bf", tag="slot_c", align_bytes=64)
+        q_bf = keep.tile([P, QT, P, PACK], BF16, name="q_bf", align_bytes=64)
         for m in range(QT):
             nc.scalar.activation(q_bf[:, m], q_by_tile[:, m], COPY)
 
         half_offsets = [offsets[:, h * NH // 16 : (h + 1) * NH // 16] for h in range(HALVES)]
 
         rk_row = keep.tile([P, N], F32, name="rk_row", align_bytes=64)
-        nc.vector.tensor_copy(rk_row[:], rk_pool[:].indirect(offsets[:]))
-        turned = psum.tile([P, N // P, P], F32, name="turned")
-        for b in range(N // P):
-            nc.tensor.transpose(turned[:, b, :], rk_row[:, b * P : (b + 1) * P], ident[:])
-        rk_col = keep.tile([P, N // P], F32, name="rk_col", tag="slot_b")
-        nc.scalar.copy(rk_col[:], turned[:, :, RK_PART])
+        rk_col = keep.tile([P, HALVES, BLOCKS], F32, name="rk_col", tag="slot_b")
         rk_all = keep.tile([P, N], F32, name="rk_all")
         for h in range(HALVES):
-            spread = psum.tile([P, BLOCKS, P], F32, name="spread%d" % h)
+            nc.vector.tensor_copy(rk_row[:, h * NH : (h + 1) * NH], rk_pool[:].indirect(half_offsets[h]))
+            turned = psum.tile([P, BLOCKS, P], F32, name="turned%d" % h, tag="turned%d" % h)
             for b in range(BLOCKS):
-                col = h * BLOCKS + b
-                nc.tensor.transpose(spread[:, b, :], rk_col[:, col : col + 1].to_broadcast([P, P]), ident[:])
+                first = h * NH + b * P
+                nc.tensor.transpose(turned[:, b, :], rk_row[:, first : first + P], ident[:])
+            nc.scalar.copy(rk_col[:, h, :], turned[:, :, RK_PART])
+        for h in range(HALVES):
+            spread = psum.tile([P, BLOCKS, P], F32, name="spread%d" % h, tag="spread%d" % h)
+            for b in range(BLOCKS):
+                nc.tensor.transpose(spread[:, b, :], rk_col[:, h, b : b + 1].to_broadcast([P, P]), ident[:])
             nc.scalar.activation(rk_all[:, h * NH : (h + 1) * NH], spread[:].rearrange("p b n -> p (b n)"), COPY, scale=10.0)
 
-        k_scale = keep.tile([P, N], U8, name="k_scale", align_bytes=64)
-        nc.vector.tensor_copy(k_scale[:], scale_pool[:].bitcast(U8).indirect(offsets[:]))
-
-        q_codes = keep.tile([P, NQ], U32, name="q_codes", tag="slot_a", align_bytes=64)
+        q_codes = reuse.tile([P, NQ], U32, name="q_codes", offset=0, align_bytes=64)
         q_scale = keep.tile([P, NQ], U8, name="q_scale", align_bytes=64)
         nc.vector.quantize_mx(
             out=q_codes[:].bitcast(FP8X4),
@@ -95,7 +102,7 @@ def tile_attend_cosexp_topk_kernel(tc, qT, k_words, k_scales, rk, rq, offs, out)
             in_=q_bf[:].rearrange("p m n j -> p (m n j)"),
         )
 
-        k_codes = keep.tile([P, N], U32, name="k_codes", tag="slot_c", align_bytes=64)
+        k_codes = reuse.tile([P, N], U32, name="k_codes", offset=4 * NQ, align_bytes=64)
         for h in range(HALVES):
             slots = slice(h * NH, (h + 1) * NH)
             nc.vector.tensor_copy(k_codes[:, slots], word_pool[:].bitcast(U32).indirect(half_offsets[h]))
@@ -105,13 +112,13 @@ def tile_attend_cosexp_topk_kernel(tc, qT, k_words, k_scales, rk, rq, offs, out)
             slots = slice(h * NH, (h + 1) * NH)
             for m in range(QT):
                 rows = slice(m * P, (m + 1) * P)
-                acc = psum.tile([P, NH], F32, name="acc%d%d" % (h, m))
+                acc = psum.tile([P, NH], F32, name="acc%d%d" % (h, m), tag=("turned1", "spread0", "spread1", "turned1")[QT * h + m])
                 nc.tensor.matmul_mx(
                     out=acc[:],
                     lhsT=q_codes[:, rows].bitcast(FP8X4),
                     lhsT_scale=q_scale[:, rows],
                     rhs=k_codes[:, slots].bitcast(FP8X4),
-                    rhs_scale=k_scale[:, slots],
+                    rhs_scale=k_scale[:].bitcast(U8)[:, slots],
                     start=True,
                     stop=True,
                 )

@@ -41,7 +41,7 @@ def tile_attend_cosexp_topk_kernel(tc, qT, k_words, k_scales, rk, rq, offs, out)
         scale_pool = keep.tile([P, T // 4], I32, name="scale_pool", align_bytes=64)
         nc.vector.memset(scale_pool[:SCALE_PART, :], 0)
         nc.vector.memset(scale_pool[64:, :], 0)
-        nc.sync.dma_start(scale_pool[SCALE_PART:64, :], k_scales[0].bitcast(I32))
+        nc.scalar.dma_start(scale_pool[SCALE_PART:64, :], k_scales[0].bitcast(I32))
 
         rk_pool = reuse.tile([P, T], F32, name="rk_pool", offset=0, align_bytes=64)
         nc.vector.memset(rk_pool[:RK_PART, :], 0.0)

@@ -71,10 +71,11 @@ def tile_attend_cosexp_topk_kernel(tc, qT, k_words, k_scales, rk, rq, offs, out)
             first = SCALE_PART + 4 * quad
             nc.sync.dma_start(k_scale[32 * quad : 32 * quad + 4, :], picked_scales[first : first + 4, :].bitcast(I32))
 
-        q_by_tile = q_raw[:].rearrange("p j (n m) -> p m n j", m=QT)
         q_bf = keep.tile([P, QT, P, PACK], BF16, name="q_bf", align_bytes=64)
-        for m in range(QT):
-            nc.scalar.activation(q_bf[:, m], q_by_tile[:, m], COPY)
+        nc.scalar.copy(
+            q_bf[:].rearrange("p m (c e) j -> p c j e m", e=2),
+            q_raw[:].rearrange("p j (c e m) -> p c j e m", e=2, m=QT),
+        )
 
         half_offsets = [offsets[:, h * NH // 16 : (h + 1) * NH // 16] for h in range(HALVES)]
 

@@ -50,11 +50,11 @@ def tile_attend_cosexp_topk_kernel(tc, qT, k_words, k_scales, rk, rq, offs, out)
         q_raw = keep.tile([P, PACK, NQ], F32, name="q_raw", tag="slot_b")
         nc.sync.dma_start(q_raw[:], qT[0].rearrange("(p j) n -> p j n", j=PACK))
 
-        word_pool = keep.tile([P, T], I32, name="word_pool", align_bytes=64)
-        nc.sync.dma_start(word_pool[:], k_words[0].rearrange("p t r -> p (t r)").bitcast(I32))
-
         rq_sb = keep.tile([P, QT], F32, name="rq_sb")
         nc.sync.dma_start(rq_sb[:], rq[0].rearrange("(p m) o -> p (m o)", m=QT))
+
+        word_pool = keep.tile([P, T], I32, name="word_pool", align_bytes=64)
+        nc.sync.dma_start(word_pool[:], k_words[0].rearrange("p t r -> p (t r)").bitcast(I32))
 
         k_zero = keep.tile([P, 1], F32, name="k_zero")
         nc.gpsimd.memset(k_zero[:], 0.0)

@@ -90,10 +90,11 @@ def tile_attend_cosexp_topk_kernel(tc, qT, k_words, k_scales, rk, rq, offs, out)
                 nc.tensor.transpose(turned[:, b, :], rk_row[:, first : first + P], ident[:])
             nc.scalar.copy(rk_col[:, h, :], turned[:, :, RK_PART])
         for h in range(HALVES):
-            spread = psum.tile([P, BLOCKS, P], F32, name="spread%d" % h, tag="spread%d" % h)
             for b in range(BLOCKS):
-                nc.tensor.transpose(spread[:, b, :], rk_col[:, h, b : b + 1].to_broadcast([P, P]), ident[:])
-            nc.scalar.activation(rk_all[:, h * NH : (h + 1) * NH], spread[:].rearrange("p b n -> p (b n)"), COPY, scale=10.0)
+                first = h * NH + b * P
+                spread = psum.tile([P, P], F32, name="spread%d%d" % (h, b), tag="spread%d%d" % (h, b))
+                nc.tensor.transpose(spread[:], rk_col[:, h, b : b + 1].to_broadcast([P, P]), ident[:])
+                nc.scalar.activation(rk_all[:, first : first + P], spread[:], COPY, scale=10.0)
 
         q_codes = reuse.tile([P, NQ], U32, name="q_codes", offset=0, align_bytes=64)
         q_scale = keep.tile([P, NQ], U8, name="q_scale", align_bytes=64)
@@ -109,26 +110,28 @@ def tile_attend_cosexp_topk_kernel(tc, qT, k_words, k_scales, rk, rq, offs, out)
             nc.vector.tensor_copy(k_codes[:, slots], word_pool[:].bitcast(U32).indirect(half_offsets[h]))
 
         out_by_tile = out[0].rearrange("(p m) n -> p m n", m=QT)
-        for h in range(HALVES):
-            slots = slice(h * NH, (h + 1) * NH)
-            for m in range(QT):
-                rows = slice(m * P, (m + 1) * P)
-                acc = psum.tile([P, NH], F32, name="acc%d%d" % (h, m), tag=("turned1", "spread0", "spread1", "turned1")[QT * h + m])
-                nc.tensor.matmul_mx(
-                    out=acc[:],
-                    lhsT=q_codes[:, rows].bitcast(FP8X4),
-                    lhsT_scale=q_scale[:, rows],
-                    rhs=k_codes[:, slots].bitcast(FP8X4),
-                    rhs_scale=k_scale[:].bitcast(U8)[:, slots],
-                    start=True,
-                    stop=True,
-                )
-                last = h == HALVES - 1 and m == QT - 1
-                width = NH // 2 if last else NH
-                for c0 in range(0, NH, width):
-                    cols = slice(c0, c0 + width)
-                    scaled = keep.tile([P, width], F32, name="scaled%d%d%d" % (h, m, c0))
-                    nc.vector.tensor_tensor(scaled[:], acc[:, cols], rk_all[:, h * NH + c0 : h * NH + c0 + width], MULT)
-                    res = keep.tile([P, width], F32, name="res%d%d%d" % (h, m, c0))
-                    nc.scalar.activation(res[:], scaled[:], EXP, bias=minus_ten[:], scale=rq_sb[:, m : m + 1])
-                    nc.sync.dma_start(out_by_tile[:, m, h * NH + c0 : h * NH + c0 + width], res[:])
+        products = (
+            (0, 0, P, "turned1"),
+            (0, P, P, "spread00"),
+            (1, 0, NH, "spread01"),
+            (0, NH, NH, "spread10"),
+            (1, NH, NH, "spread11"),
+        )
+        for m, first, width, bank in products:
+            rows = slice(m * P, (m + 1) * P)
+            slots = slice(first, first + width)
+            acc = psum.tile([P, width], F32, name="acc%d_%d" % (m, first), tag=bank)
+            nc.tensor.matmul_mx(
+                out=acc[:],
+                lhsT=q_codes[:, rows].bitcast(FP8X4),
+                lhsT_scale=q_scale[:, rows],
+                rhs=k_codes[:, slots].bitcast(FP8X4),
+                rhs_scale=k_scale[:].bitcast(U8)[:, slots],
+                start=True,
+                stop=True,
+            )
+            scaled = keep.tile([P, width], F32, name="scaled%d_%d" % (m, first))
+            nc.vector.tensor_tensor(scaled[:], acc[:], rk_all[:, slots], MULT)
+            res = keep.tile([P, width], F32, name="res%d_%d" % (m, first))
+            nc.scalar.activation(res[:], scaled[:], EXP, bias=minus_ten[:], scale=rq_sb[:, m : m + 1])
+            nc.sync.dma_start(out_by_tile[:, m, slots], res[:])

@@ -26,6 +26,7 @@ BLOCKS = NH // P
 RK_PART = P - 1
 SCALE_ROWS = D // 32
 SCALE_PART = 64 - SCALE_ROWS
+BANK = 2048
 
 
 def tile_attend_cosexp_topk_kernel(tc, qT, k_words, k_scales, rk, rq, offs, out):
@@ -84,7 +85,7 @@ def tile_attend_cosexp_topk_kernel(tc, qT, k_words, k_scales, rk, rq, offs, out)
         rk_all = keep.tile([P, N], F32, name="rk_all")
         for h in range(HALVES):
             nc.vector.tensor_copy(rk_row[:, h * NH : (h + 1) * NH], rk_pool[:].indirect(half_offsets[h]))
-            turned = psum.tile([P, BLOCKS, P], F32, name="turned%d" % h, tag="turned%d" % h)
+            turned = psum.tile([P, BLOCKS, P], F32, name="turned%d" % h, offset=BANK * (7, 0)[h])
             for b in range(BLOCKS):
                 first = h * NH + b * P
                 nc.tensor.transpose(turned[:, b, :], rk_row[:, first : first + P], ident[:])
@@ -92,9 +93,11 @@ def tile_attend_cosexp_topk_kernel(tc, qT, k_words, k_scales, rk, rq, offs, out)
         for h in range(HALVES):
             for b in range(BLOCKS):
                 first = h * NH + b * P
-                spread = psum.tile([P, P], F32, name="spread%d%d" % (h, b), tag="spread%d%d" % (h, b))
-                nc.tensor.transpose(spread[:], rk_col[:, h, b : b + 1].to_broadcast([P, P]), ident[:])
-                nc.scalar.activation(rk_all[:, first : first + P], spread[:], COPY, scale=10.0)
+                block = BLOCKS * h + b
+                banks = 4 if block == 3 else 1
+                spread = psum.tile([P, banks * BANK // 4], F32, name="spread%d" % block, offset=BANK * (1 + block))
+                nc.tensor.transpose(spread[:, :P], rk_col[:, h, b : b + 1].to_broadcast([P, P]), ident[:])
+                nc.scalar.activation(rk_all[:, first : first + P], spread[:, :P], COPY, scale=10.0)
 
         q_codes = reuse.tile([P, NQ], U32, name="q_codes", offset=0, align_bytes=64)
         q_scale = keep.tile([P, NQ], U8, name="q_scale", align_bytes=64)
@@ -110,28 +113,28 @@ def tile_attend_cosexp_topk_kernel(tc, qT, k_words, k_scales, rk, rq, offs, out)
             nc.vector.tensor_copy(k_codes[:, slots], word_pool[:].bitcast(U32).indirect(half_offsets[h]))
 
         out_by_tile = out[0].rearrange("(p m) n -> p m n", m=QT)
-        products = (
-            (0, 0, P, "turned1"),
-            (0, P, P, "spread00"),
-            (1, 0, NH, "spread01"),
-            (0, NH, NH, "spread10"),
-            (1, NH, NH, "spread11"),
-        )
-        for m, first, width, bank in products:
-            rows = slice(m * P, (m + 1) * P)
-            slots = slice(first, first + width)
-            acc = psum.tile([P, width], F32, name="acc%d_%d" % (m, first), tag=bank)
-            nc.tensor.matmul_mx(
-                out=acc[:],
-                lhsT=q_codes[:, rows].bitcast(FP8X4),
-                lhsT_scale=q_scale[:, rows],
-                rhs=k_codes[:, slots].bitcast(FP8X4),
-                rhs_scale=k_scale[:].bitcast(U8)[:, slots],
-                start=True,
-                stop=True,
-            )
-            scaled = keep.tile([P, width], F32, name="scaled%d_%d" % (m, first))
-            nc.vector.tensor_tensor(scaled[:], acc[:], rk_all[:, slots], MULT)
-            res = keep.tile([P, width], F32, name="res%d_%d" % (m, first))
-            nc.scalar.activation(res[:], scaled[:], EXP, bias=minus_ten[:], scale=rq_sb[:, m : m + 1])
-            nc.sync.dma_start(out_by_tile[:, m, slots], res[:])
+        for h in range(HALVES):
+            for m in range(QT):
+                rows = slice(m * P, (m + 1) * P)
+                res = keep.tile([P, NH], F32, name="res%d%d" % (h, m))
+                for b in range(BLOCKS):
+                    step = (h * QT + m) * BLOCKS + b
+                    slots = slice(h * NH + b * P, h * NH + (b + 1) * P)
+                    cols = slice(b * P, (b + 1) * P)
+                    acc = psum.tile([P, P], F32, name="acc%d" % step, offset=BANK * step)
+                    nc.tensor.matmul_mx(
+                        out=acc[:],
+                        lhsT=q_codes[:, rows].bitcast(FP8X4),
+                        lhsT_scale=q_scale[:, rows],
+                        rhs=k_codes[:, slots].bitcast(FP8X4),
+                        rhs_scale=k_scale[:].bitcast(U8)[:, slots],
+                        start=True,
+                        stop=True,
+                    )
+                    scaled = keep.tile([P, P], F32, name="scaled%d" % step)
+                    nc.vector.tensor_tensor(scaled[:], acc[:], rk_all[:, slots], MULT)
+                    nc.scalar.activation(res[:, cols], scaled[:], EXP, bias=minus_ten[:], scale=rq_sb[:, m : m + 1])
+                    if h == 0 and m == 0:
+                        nc.sync.dma_start(out_by_tile[:, m, slots], res[:, cols])
+                if h > 0 or m > 0:
+                    nc.sync.dma_start(out_by_tile[:, m, h * NH : (h + 1) * NH], res[:])

@@ -39,6 +39,10 @@ def tile_attend_cosexp_topk_kernel(tc, qT, k_words, k_scales, rk, rq, offs, out)
         offsets = keep.tile([P, N // 16], U16, name="offsets")
         nc.sync.dma_start(offsets[:], offs)
 
+        ident = keep.tile([P, P], F32, name="ident")
+        nc.vector.memset(ident[:], 0.0)
+        make_identity(nc, ident[:], nomemset=True)
+
         scale_pool = keep.tile([P, T // 4], I32, name="scale_pool", align_bytes=64)
         nc.vector.memset(scale_pool[:SCALE_PART, :], 0)
         nc.vector.memset(scale_pool[64:, :], 0)
@@ -57,14 +61,10 @@ def tile_attend_cosexp_topk_kernel(tc, qT, k_words, k_scales, rk, rq, offs, out)
         word_pool = keep.tile([P, T], I32, name="word_pool", align_bytes=64)
         nc.sync.dma_start(word_pool[:], k_words[0].rearrange("p t r -> p (t r)").bitcast(I32))
 
-        k_zero = keep.tile([P, 1], F32, name="k_zero")
-        nc.gpsimd.memset(k_zero[:], 0.0)
         k_scale = keep.tile([P, N // 4], I32, name="k_scale", align_bytes=64)
-        nc.gpsimd.memset(k_scale[:], 0)
-        ident = keep.tile([P, P], F32, name="ident")
-        make_identity(nc, ident[:])
+        nc.vector.memset(k_scale[:], 0)
         minus_ten = keep.tile([P, 1], F32, name="minus_ten")
-        nc.scalar.activation(minus_ten[:], k_zero[:], COPY, bias=-10.0)
+        nc.scalar.activation(minus_ten[:], ident[:, 0:1], COPY, bias=-10.0, scale=0.0)
 
         picked_scales = keep.tile([P, N], U8, name="picked_scales", align_bytes=64)
         nc.vector.tensor_copy(picked_scales[:], scale_pool[:].bitcast(U8).indirect(offsets[:]))
@@ -85,19 +85,18 @@ def tile_attend_cosexp_topk_kernel(tc, qT, k_words, k_scales, rk, rq, offs, out)
         rk_all = keep.tile([P, N], F32, name="rk_all")
         for h in range(HALVES):
             nc.vector.tensor_copy(rk_row[:, h * NH : (h + 1) * NH], rk_pool[:].indirect(half_offsets[h]))
-            turned = psum.tile([P, BLOCKS, P], F32, name="turned%d" % h, offset=BANK * (7, 0)[h])
+            turned = psum.tile([P, (BLOCKS, 4 * BANK // (4 * P))[h], P], F32, name="turned%d" % h, offset=BANK * (6, 0)[h])
             for b in range(BLOCKS):
                 first = h * NH + b * P
                 nc.tensor.transpose(turned[:, b, :], rk_row[:, first : first + P], ident[:])
-            nc.scalar.copy(rk_col[:, h, :], turned[:, :, RK_PART])
+            nc.scalar.copy(rk_col[:, h, :], turned[:, :BLOCKS, RK_PART])
         for h in range(HALVES):
             for b in range(BLOCKS):
                 first = h * NH + b * P
                 block = BLOCKS * h + b
-                banks = 4 if block == 3 else 1
-                spread = psum.tile([P, banks * BANK // 4], F32, name="spread%d" % block, offset=BANK * (1 + block))
-                nc.tensor.transpose(spread[:, :P], rk_col[:, h, b : b + 1].to_broadcast([P, P]), ident[:])
-                nc.scalar.activation(rk_all[:, first : first + P], spread[:, :P], COPY, scale=10.0)
+                spread = psum.tile([P, P], F32, name="spread%d" % block, offset=BANK * (4 + block))
+                nc.tensor.transpose(spread[:], rk_col[:, h, b : b + 1].to_broadcast([P, P]), ident[:])
+                nc.scalar.activation(rk_all[:, first : first + P], spread[:], COPY, scale=10.0)
 
         q_codes = reuse.tile([P, NQ], U32, name="q_codes", offset=0, align_bytes=64)
         q_scale = keep.tile([P, NQ], U8, name="q_scale", align_bytes=64)

@@ -33,7 +33,6 @@ def tile_attend_cosexp_topk_kernel(tc, qT, k_words, k_scales, rk, rq, offs, out)
     nc = tc.nc
     with ExitStack() as ctx:
         keep = ctx.enter_context(tc.tile_pool(name="keep", bufs=1))
-        reuse = ctx.enter_context(tc.tile_pool(name="reuse", bufs=1))
         psum = ctx.enter_context(tc.psum_pool(name="psum", bufs=1))
 
         offsets = keep.tile([P, N // 16], U16, name="offsets")
@@ -48,11 +47,11 @@ def tile_attend_cosexp_topk_kernel(tc, qT, k_words, k_scales, rk, rq, offs, out)
         nc.vector.memset(scale_pool[64:, :], 0)
         nc.scalar.dma_start(scale_pool[SCALE_PART:64, :], k_scales[0].bitcast(I32))
 
-        rk_pool = reuse.tile([P, T], F32, name="rk_pool", offset=0, align_bytes=64)
+        rk_pool = keep.tile([P, T], F32, name="rk_pool", align_bytes=64)
         nc.vector.memset(rk_pool[:RK_PART, :], 0.0)
         nc.scalar.dma_start(rk_pool[RK_PART : RK_PART + 1, :], rk[0:1, :])
 
-        q_raw = keep.tile([P, PACK, NQ], F32, name="q_raw", tag="slot_b")
+        q_raw = keep.tile([P, PACK, NQ], F32, name="q_raw")
         nc.sync.dma_start(q_raw[:], qT[0].rearrange("(p j) n -> p j n", j=PACK))
 
         rq_sb = keep.tile([P, QT], F32, name="rq_sb")
@@ -64,7 +63,9 @@ def tile_attend_cosexp_topk_kernel(tc, qT, k_words, k_scales, rk, rq, offs, out)
         k_scale = keep.tile([P, N // 4], I32, name="k_scale", align_bytes=64)
         nc.vector.memset(k_scale[:], 0)
         minus_ten = keep.tile([P, 1], F32, name="minus_ten")
-        nc.scalar.activation(minus_ten[:], ident[:, 0:1], COPY, bias=-10.0, scale=0.0)
+        zero = keep.tile([P, 1], F32, name="zero")
+        nc.gpsimd.memset(zero[:], 0.0)
+        nc.scalar.activation(minus_ten[:], zero[:], COPY, bias=-10.0)
 
         picked_scales = keep.tile([P, N], U8, name="picked_scales", align_bytes=64)
         nc.vector.tensor_copy(picked_scales[:], scale_pool[:].bitcast(U8).indirect(offsets[:]))
@@ -73,7 +74,7 @@ def tile_attend_cosexp_topk_kernel(tc, qT, k_words, k_scales, rk, rq, offs, out)
             nc.sync.dma_start(k_scale[32 * quad : 32 * quad + 4, :], picked_scales[first : first + 4, :].bitcast(I32))
 
         q_bf = keep.tile([P, QT, P, PACK], BF16, name="q_bf", align_bytes=64)
-        nc.scalar.copy(
+        nc.vector.tensor_copy(
             q_bf[:].rearrange("p m (c e) j -> p c j e m", e=2),
             q_raw[:].rearrange("p j (c e m) -> p c j e m", e=2, m=QT),
         )
@@ -81,10 +82,10 @@ def tile_attend_cosexp_topk_kernel(tc, qT, k_words, k_scales, rk, rq, offs, out)
         half_offsets = [offsets[:, h * NH // 16 : (h + 1) * NH // 16] for h in range(HALVES)]
 
         rk_row = keep.tile([P, N], F32, name="rk_row", align_bytes=64)
-        rk_col = keep.tile([P, HALVES, BLOCKS], F32, name="rk_col", tag="slot_b")
+        rk_col = keep.tile([P, HALVES, BLOCKS], F32, name="rk_col")
         rk_all = keep.tile([P, N], F32, name="rk_all")
         for h in range(HALVES):
-            nc.vector.tensor_copy(rk_row[:, h * NH : (h + 1) * NH], rk_pool[:].indirect(half_offsets[h]))
+            nc.scalar.activation(rk_row[:, h * NH : (h + 1) * NH], rk_pool[:].indirect(half_offsets[h]), COPY)
             turned = psum.tile([P, (BLOCKS, 4 * BANK // (4 * P))[h], P], F32, name="turned%d" % h, offset=BANK * (6, 0)[h])
             for b in range(BLOCKS):
                 first = h * NH + b * P
@@ -98,7 +99,7 @@ def tile_attend_cosexp_topk_kernel(tc, qT, k_words, k_scales, rk, rq, offs, out)
                 nc.tensor.transpose(spread[:], rk_col[:, h, b : b + 1].to_broadcast([P, P]), ident[:])
                 nc.scalar.activation(rk_all[:, first : first + P], spread[:], COPY, scale=10.0)
 
-        q_codes = reuse.tile([P, NQ], U32, name="q_codes", offset=0, align_bytes=64)
+        q_codes = keep.tile([P, NQ], U32, name="q_codes", align_bytes=64)
         q_scale = keep.tile([P, NQ], U8, name="q_scale", align_bytes=64)
         nc.vector.quantize_mx(
             out=q_codes[:].bitcast(FP8X4),
@@ -106,10 +107,11 @@ def tile_attend_cosexp_topk_kernel(tc, qT, k_words, k_scales, rk, rq, offs, out)
             in_=q_bf[:].rearrange("p m n j -> p (m n j)"),
         )
 
-        k_codes = reuse.tile([P, N], U32, name="k_codes", offset=4 * NQ, align_bytes=64)
-        for h in range(HALVES):
-            slots = slice(h * NH, (h + 1) * NH)
-            nc.vector.tensor_copy(k_codes[:, slots], word_pool[:].bitcast(U32).indirect(half_offsets[h]))
+        k_codes = keep.tile([P, N], U32, name="k_codes", align_bytes=64)
+        for first, last in ((0, P), (P, NH), (NH, N)):
+            nc.vector.tensor_copy(
+                k_codes[:, first:last], word_pool[:].bitcast(U32).indirect(offsets[:, first // 16 : last // 16])
+            )
 
         out_by_tile = out[0].rearrange("(p m) n -> p m n", m=QT)
         for h in range(HALVES):

@@ -42,14 +42,14 @@ def tile_attend_cosexp_topk_kernel(tc, qT, k_words, k_scales, rk, rq, offs, out)
         nc.vector.memset(ident[:], 0.0)
         make_identity(nc, ident[:], nomemset=True)
 
-        scale_pool = keep.tile([P, T // 4], I32, name="scale_pool", align_bytes=64)
-        nc.vector.memset(scale_pool[:SCALE_PART, :], 0)
-        nc.vector.memset(scale_pool[64:, :], 0)
-        nc.scalar.dma_start(scale_pool[SCALE_PART:64, :], k_scales[0].bitcast(I32))
-
         rk_pool = keep.tile([P, T], F32, name="rk_pool", align_bytes=64)
         nc.vector.memset(rk_pool[:RK_PART, :], 0.0)
         nc.scalar.dma_start(rk_pool[RK_PART : RK_PART + 1, :], rk[0:1, :])
+
+        scale_pool = keep.tile([P, T // 4], I32, name="scale_pool", align_bytes=64)
+        nc.vector.memset(scale_pool[:SCALE_PART, :], 0)
+        nc.vector.memset(scale_pool[64:, :], 0)
+        nc.sync.dma_start(scale_pool[SCALE_PART:64, :], k_scales[0].bitcast(I32))
 
         q_raw = keep.tile([P, PACK, NQ], F32, name="q_raw")
         nc.sync.dma_start(q_raw[:], qT[0].rearrange("(p j) n -> p j n", j=PACK))

@@ -38,21 +38,23 @@ def tile_attend_cosexp_topk_kernel(tc, qT, k_words, k_scales, rk, rq, offs, out)
         offsets = keep.tile([P, N // 16], U16, name="offsets")
         nc.sync.dma_start(offsets[:], offs)
 
+        zero = keep.tile([P, 1], F32, name="zero")
+        nc.vector.memset(zero[:], 0.0)
         ident = keep.tile([P, P], F32, name="ident")
         nc.vector.memset(ident[:], 0.0)
         make_identity(nc, ident[:], nomemset=True)
 
         rk_pool = keep.tile([P, T], F32, name="rk_pool", align_bytes=64)
         nc.vector.memset(rk_pool[:RK_PART, :], 0.0)
-        nc.scalar.dma_start(rk_pool[RK_PART : RK_PART + 1, :], rk[0:1, :])
+        nc.sync.dma_start(rk_pool[RK_PART : RK_PART + 1, :], rk[0:1, :])
 
         scale_pool = keep.tile([P, T // 4], I32, name="scale_pool", align_bytes=64)
         nc.vector.memset(scale_pool[:SCALE_PART, :], 0)
         nc.vector.memset(scale_pool[64:, :], 0)
-        nc.sync.dma_start(scale_pool[SCALE_PART:64, :], k_scales[0].bitcast(I32))
+        nc.scalar.dma_start(scale_pool[SCALE_PART:64, :], k_scales[0].bitcast(I32))
 
         q_raw = keep.tile([P, PACK, NQ], F32, name="q_raw")
-        nc.sync.dma_start(q_raw[:], qT[0].rearrange("(p j) n -> p j n", j=PACK))
+        nc.scalar.dma_start(q_raw[:], qT[0].rearrange("(p j) n -> p j n", j=PACK))
 
         rq_sb = keep.tile([P, QT], F32, name="rq_sb")
         nc.sync.dma_start(rq_sb[:], rq[0].rearrange("(p m) o -> p (m o)", m=QT))
@@ -63,9 +65,29 @@ def tile_attend_cosexp_topk_kernel(tc, qT, k_words, k_scales, rk, rq, offs, out)
         k_scale = keep.tile([P, N // 4], I32, name="k_scale", align_bytes=64)
         nc.vector.memset(k_scale[:], 0)
         minus_ten = keep.tile([P, 1], F32, name="minus_ten")
-        zero = keep.tile([P, 1], F32, name="zero")
-        nc.gpsimd.memset(zero[:], 0.0)
         nc.scalar.activation(minus_ten[:], zero[:], COPY, bias=-10.0)
+
+        pieces = ((0, P), (P, NH), (NH, N))
+
+        rk_col = keep.tile([P, HALVES, BLOCKS], F32, name="rk_col")
+        rk_all = keep.tile([P, N], F32, name="rk_all")
+        rk_rows = []
+        for first, last in pieces:
+            rk_row = keep.tile([P, last - first], F32, name="rk_row%d" % first, align_bytes=64)
+            nc.scalar.activation(rk_row[:], rk_pool[:].indirect(offsets[:, first // 16 : last // 16]), COPY)
+            rk_rows.extend(rk_row[:, c : c + P] for c in range(0, last - first, P))
+        for h in range(HALVES):
+            turned = psum.tile([P, (BLOCKS, 4 * BANK // (4 * P))[h], P], F32, name="turned%d" % h, offset=BANK * (6, 0)[h])
+            for b in range(BLOCKS):
+                nc.tensor.transpose(turned[:, b, :], rk_rows[BLOCKS * h + b], ident[:])
+            nc.scalar.copy(rk_col[:, h, :], turned[:, :BLOCKS, RK_PART])
+        for h in range(HALVES):
+            for b in range(BLOCKS):
+                first = h * NH + b * P
+                block = BLOCKS * h + b
+                spread = psum.tile([P, P], F32, name="spread%d" % block, offset=BANK * (4 + block))
+                nc.tensor.transpose(spread[:], rk_col[:, h, b : b + 1].to_broadcast([P, P]), ident[:])
+                nc.scalar.activation(rk_all[:, first : first + P], spread[:], COPY, scale=10.0)
 
         picked_scales = keep.tile([P, N], U8, name="picked_scales", align_bytes=64)
         nc.vector.tensor_copy(picked_scales[:], scale_pool[:].bitcast(U8).indirect(offsets[:]))
@@ -79,26 +101,6 @@ def tile_attend_cosexp_topk_kernel(tc, qT, k_words, k_scales, rk, rq, offs, out)
             q_raw[:].rearrange("p j (c e m) -> p c j e m", e=2, m=QT),
         )
 
-        half_offsets = [offsets[:, h * NH // 16 : (h + 1) * NH // 16] for h in range(HALVES)]
-
-        rk_row = keep.tile([P, N], F32, name="rk_row", align_bytes=64)
-        rk_col = keep.tile([P, HALVES, BLOCKS], F32, name="rk_col")
-        rk_all = keep.tile([P, N], F32, name="rk_all")
-        for h in range(HALVES):
-            nc.scalar.activation(rk_row[:, h * NH : (h + 1) * NH], rk_pool[:].indirect(half_offsets[h]), COPY)
-            turned = psum.tile([P, (BLOCKS, 4 * BANK // (4 * P))[h], P], F32, name="turned%d" % h, offset=BANK * (6, 0)[h])
-            for b in range(BLOCKS):
-                first = h * NH + b * P
-                nc.tensor.transpose(turned[:, b, :], rk_row[:, first : first + P], ident[:])
-            nc.scalar.copy(rk_col[:, h, :], turned[:, :BLOCKS, RK_PART])
-        for h in range(HALVES):
-            for b in range(BLOCKS):
-                first = h * NH + b * P
-                block = BLOCKS * h + b
-                spread = psum.tile([P, P], F32, name="spread%d" % block, offset=BANK * (4 + block))
-                nc.tensor.transpose(spread[:], rk_col[:, h, b : b + 1].to_broadcast([P, P]), ident[:])
-                nc.scalar.activation(rk_all[:, first : first + P], spread[:], COPY, scale=10.0)
-
         q_codes = keep.tile([P, NQ], U32, name="q_codes", align_bytes=64)
         q_scale = keep.tile([P, NQ], U8, name="q_scale", align_bytes=64)
         nc.vector.quantize_mx(
@@ -108,34 +110,33 @@ def tile_attend_cosexp_topk_kernel(tc, qT, k_words, k_scales, rk, rq, offs, out)
         )
 
         k_codes = keep.tile([P, N], U32, name="k_codes", align_bytes=64)
-        for first, last in ((0, P), (P, NH), (NH, N)):
+        for first in range(0, N, P):
             nc.vector.tensor_copy(
-                k_codes[:, first:last], word_pool[:].bitcast(U32).indirect(offsets[:, first // 16 : last // 16])
+                k_codes[:, first : first + P],
+                word_pool[:].bitcast(U32).indirect(offsets[:, first // 16 : (first + P) // 16]),
             )
 
         out_by_tile = out[0].rearrange("(p m) n -> p m n", m=QT)
-        for h in range(HALVES):
+        for block in range(N // P):
+            slots = slice(block * P, (block + 1) * P)
+            res = keep.tile([P, QT, P], F32, name="res%d" % block)
             for m in range(QT):
                 rows = slice(m * P, (m + 1) * P)
-                res = keep.tile([P, NH], F32, name="res%d%d" % (h, m))
-                for b in range(BLOCKS):
-                    step = (h * QT + m) * BLOCKS + b
-                    slots = slice(h * NH + b * P, h * NH + (b + 1) * P)
-                    cols = slice(b * P, (b + 1) * P)
-                    acc = psum.tile([P, P], F32, name="acc%d" % step, offset=BANK * step)
-                    nc.tensor.matmul_mx(
-                        out=acc[:],
-                        lhsT=q_codes[:, rows].bitcast(FP8X4),
-                        lhsT_scale=q_scale[:, rows],
-                        rhs=k_codes[:, slots].bitcast(FP8X4),
-                        rhs_scale=k_scale[:].bitcast(U8)[:, slots],
-                        start=True,
-                        stop=True,
-                    )
-                    scaled = keep.tile([P, P], F32, name="scaled%d" % step)
-                    nc.vector.tensor_tensor(scaled[:], acc[:], rk_all[:, slots], MULT)
-                    nc.scalar.activation(res[:, cols], scaled[:], EXP, bias=minus_ten[:], scale=rq_sb[:, m : m + 1])
-                    if h == 0 and m == 0:
-                        nc.sync.dma_start(out_by_tile[:, m, slots], res[:, cols])
-                if h > 0 or m > 0:
-                    nc.sync.dma_start(out_by_tile[:, m, h * NH : (h + 1) * NH], res[:])
+                step = block * QT + m
+                acc = psum.tile([P, P], F32, name="acc%d" % step, offset=BANK * step)
+                nc.tensor.matmul_mx(
+                    out=acc[:],
+                    lhsT=q_codes[:, rows].bitcast(FP8X4),
+                    lhsT_scale=q_scale[:, rows],
+                    rhs=k_codes[:, slots].bitcast(FP8X4),
+                    rhs_scale=k_scale[:].bitcast(U8)[:, slots],
+                    start=True,
+                    stop=True,
+                )
+                scaled = keep.tile([P, P], F32, name="scaled%d" % step)
+                nc.vector.tensor_tensor(scaled[:], acc[:], rk_all[:, slots], MULT)
+                nc.scalar.activation(res[:, m, :], scaled[:], EXP, bias=minus_ten[:], scale=rq_sb[:, m : m + 1])
+                if block == 0:
+                    nc.sync.dma_start(out_by_tile[:, m, slots], res[:, m, :])
+            if block > 0:
+                nc.sync.dma_start(out_by_tile[:, :, slots], res[:])

@@ -56,8 +56,9 @@ def tile_attend_cosexp_topk_kernel(tc, qT, k_words, k_scales, rk, rq, offs, out)
         q_raw = keep.tile([P, PACK, NQ], F32, name="q_raw")
         nc.scalar.dma_start(q_raw[:], qT[0].rearrange("(p j) n -> p j n", j=PACK))
 
-        rq_sb = keep.tile([P, QT], F32, name="rq_sb")
-        nc.sync.dma_start(rq_sb[:], rq[0].rearrange("(p m) o -> p (m o)", m=QT))
+        rq_rows = keep.tile([P, P], F32, name="rq_rows")
+        nc.vector.memset(rq_rows[: P - QT, :], 0.0)
+        nc.sync.dma_start(rq_rows[P - QT :, :], rq[0].rearrange("(m p) o -> m (p o)", m=QT))
 
         word_pool = keep.tile([P, T], I32, name="word_pool", align_bytes=64)
         nc.sync.dma_start(word_pool[:], k_words[0].rearrange("p t r -> p (t r)").bitcast(I32))
@@ -89,16 +90,21 @@ def tile_attend_cosexp_topk_kernel(tc, qT, k_words, k_scales, rk, rq, offs, out)
                 nc.tensor.transpose(spread[:], rk_col[:, h, b : b + 1].to_broadcast([P, P]), ident[:])
                 nc.scalar.activation(rk_all[:, first : first + P], spread[:], COPY, scale=10.0)
 
+        rq_turned = psum.tile([P, P], F32, name="rq_turned", offset=BANK * 5)
+        nc.tensor.transpose(rq_turned[:], rq_rows[:], ident[:])
+        rq_sb = keep.tile([P, QT], F32, name="rq_sb")
+        nc.scalar.copy(rq_sb[:], rq_turned[:, P - QT :])
+
         picked_scales = keep.tile([P, N], U8, name="picked_scales", align_bytes=64)
         nc.vector.tensor_copy(picked_scales[:], scale_pool[:].bitcast(U8).indirect(offsets[:]))
         for quad in range(4):
             first = SCALE_PART + 4 * quad
             nc.sync.dma_start(k_scale[32 * quad : 32 * quad + 4, :], picked_scales[first : first + 4, :].bitcast(I32))
 
-        q_bf = keep.tile([P, QT, P, PACK], BF16, name="q_bf", align_bytes=64)
+        q_bf = keep.tile([P, NQ, PACK], BF16, name="q_bf", align_bytes=64)
         nc.vector.tensor_copy(
-            q_bf[:].rearrange("p m (c e) j -> p c j e m", e=2),
-            q_raw[:].rearrange("p j (c e m) -> p c j e m", e=2, m=QT),
+            q_bf[:].rearrange("p (c i) j -> p c j i", i=4),
+            q_raw[:].rearrange("p j (c i) -> p c j i", i=4),
         )
 
         q_codes = keep.tile([P, NQ], U32, name="q_codes", align_bytes=64)
@@ -106,7 +112,7 @@ def tile_attend_cosexp_topk_kernel(tc, qT, k_words, k_scales, rk, rq, offs, out)
         nc.vector.quantize_mx(
             out=q_codes[:].bitcast(FP8X4),
             scales=q_scale[:],
-            in_=q_bf[:].rearrange("p m n j -> p (m n j)"),
+            in_=q_bf[:].rearrange("p n j -> p (n j)"),
         )
 
         k_codes = keep.tile([P, N], U32, name="k_codes", align_bytes=64)
@@ -116,7 +122,7 @@ def tile_attend_cosexp_topk_kernel(tc, qT, k_words, k_scales, rk, rq, offs, out)
                 word_pool[:].bitcast(U32).indirect(offsets[:, first // 16 : (first + P) // 16]),
             )
 
-        out_by_tile = out[0].rearrange("(p m) n -> p m n", m=QT)
+        out_by_tile = out[0].rearrange("(m p) n -> p m n", m=QT)
         for block in range(N // P):
             slots = slice(block * P, (block + 1) * P)
             res = keep.tile([P, QT, P], F32, name="res%d" % block)

@@ -1,7 +1,6 @@
 from contextlib import ExitStack
 
 import concourse.mybir as mybir
-from concourse.masks import make_identity
 
 D, NQ, N, T = 512, 256, 512, 2048
 FLOPS = 2 * D * NQ * N
@@ -16,6 +15,7 @@ FP8X4 = mybir.dt.float8_e4m3fn_x4
 EXP = mybir.ActivationFunctionType.Exp
 COPY = mybir.ActivationFunctionType.Copy
 MULT = mybir.AluOpType.mult
+NOT_EQUAL = mybir.AluOpType.not_equal
 
 P = 128
 PACK = 4
@@ -27,22 +27,39 @@ RK_PART = P - 1
 SCALE_ROWS = D // 32
 SCALE_PART = 64 - SCALE_ROWS
 BANK = 2048
+LAST_COLS = 16
 
 
 def tile_attend_cosexp_topk_kernel(tc, qT, k_words, k_scales, rk, rq, offs, out):
     nc = tc.nc
     with ExitStack() as ctx:
         keep = ctx.enter_context(tc.tile_pool(name="keep", bufs=1))
+        reuse = ctx.enter_context(tc.tile_pool(name="reuse", bufs=1))
         psum = ctx.enter_context(tc.psum_pool(name="psum", bufs=1))
 
         offsets = keep.tile([P, N // 16], U16, name="offsets")
         nc.sync.dma_start(offsets[:], offs)
 
+        ident = keep.tile([P, P], F32, name="ident")
+
+        def identity_columns(zeros, first, count):
+            nc.gpsimd.affine_select(
+                out=ident[:, first : first + count],
+                in_=zeros,
+                pattern=[[-1, count]],
+                compare_op=NOT_EQUAL,
+                fill=1.0,
+                base=-first,
+                channel_multiplier=1,
+            )
+
         zero = keep.tile([P, 1], F32, name="zero")
         nc.vector.memset(zero[:], 0.0)
-        ident = keep.tile([P, P], F32, name="ident")
-        nc.vector.memset(ident[:], 0.0)
-        make_identity(nc, ident[:], nomemset=True)
+        wide_zero = reuse.tile([P, P - LAST_COLS], F32, name="wide_zero", offset=8 * LAST_COLS, align_bytes=64)
+        nc.vector.memset(wide_zero[:], 0.0)
+        identity_columns(wide_zero[:], 0, P - LAST_COLS)
+        k_scale = reuse.tile([P, N // 4], I32, name="k_scale", offset=0, align_bytes=64)
+        nc.gpsimd.memset(k_scale[:], 0)
 
         rk_pool = keep.tile([P, T], F32, name="rk_pool", align_bytes=64)
         nc.vector.memset(rk_pool[:RK_PART, :], 0.0)
@@ -63,10 +80,12 @@ def tile_attend_cosexp_topk_kernel(tc, qT, k_words, k_scales, rk, rq, offs, out)
         word_pool = keep.tile([P, T], I32, name="word_pool", align_bytes=64)
         nc.sync.dma_start(word_pool[:], k_words[0].rearrange("p t r -> p (t r)").bitcast(I32))
 
-        k_scale = keep.tile([P, N // 4], I32, name="k_scale", align_bytes=64)
-        nc.vector.memset(k_scale[:], 0)
         minus_ten = keep.tile([P, 1], F32, name="minus_ten")
         nc.scalar.activation(minus_ten[:], zero[:], COPY, bias=-10.0)
+
+        last_zero = reuse.tile([P, LAST_COLS], F32, name="last_zero", offset=N, align_bytes=64)
+        nc.gpsimd.memset(last_zero[:], 0.0)
+        identity_columns(last_zero[:], P - LAST_COLS, LAST_COLS)
 
         pieces = ((0, P), (P, NH), (NH, N))
 
@@ -82,6 +101,11 @@ def tile_attend_cosexp_topk_kernel(tc, qT, k_words, k_scales, rk, rq, offs, out)
             for b in range(BLOCKS):
                 nc.tensor.transpose(turned[:, b, :], rk_rows[BLOCKS * h + b], ident[:])
             nc.scalar.copy(rk_col[:, h, :], turned[:, :BLOCKS, RK_PART])
+        rq_turned = psum.tile([P, P], F32, name="rq_turned", offset=BANK * 7)
+        nc.tensor.transpose(rq_turned[:], rq_rows[:], ident[:])
+        rq_sb = keep.tile([P, QT], F32, name="rq_sb")
+        nc.scalar.copy(rq_sb[:], rq_turned[:, P - QT :])
+
         for h in range(HALVES):
             for b in range(BLOCKS):
                 first = h * NH + b * P
@@ -90,16 +114,12 @@ def tile_attend_cosexp_topk_kernel(tc, qT, k_words, k_scales, rk, rq, offs, out)
                 nc.tensor.transpose(spread[:], rk_col[:, h, b : b + 1].to_broadcast([P, P]), ident[:])
                 nc.scalar.activation(rk_all[:, first : first + P], spread[:], COPY, scale=10.0)
 
-        rq_turned = psum.tile([P, P], F32, name="rq_turned", offset=BANK * 5)
-        nc.tensor.transpose(rq_turned[:], rq_rows[:], ident[:])
-        rq_sb = keep.tile([P, QT], F32, name="rq_sb")
-        nc.scalar.copy(rq_sb[:], rq_turned[:, P - QT :])
-
         picked_scales = keep.tile([P, N], U8, name="picked_scales", align_bytes=64)
         nc.vector.tensor_copy(picked_scales[:], scale_pool[:].bitcast(U8).indirect(offsets[:]))
         for quad in range(4):
             first = SCALE_PART + 4 * quad
-            nc.sync.dma_start(k_scale[32 * quad : 32 * quad + 4, :], picked_scales[first : first + 4, :].bitcast(I32))
+            queue = (nc.sync, nc.scalar)[quad % 2]
+            queue.dma_start(k_scale[32 * quad : 32 * quad + 4, :], picked_scales[first : first + 4, :].bitcast(I32))
 
         q_bf = keep.tile([P, NQ, PACK], BF16, name="q_bf", align_bytes=64)
         nc.vector.tensor_copy(

@@ -61,7 +61,7 @@ def tile_attend_cosexp_topk_kernel(tc, qT, k_words, k_scales, rk, rq, offs, out)
         k_scale = reuse.tile([P, N // 4], I32, name="k_scale", offset=0, align_bytes=64)
         nc.gpsimd.memset(k_scale[:], 0)
 
-        rk_pool = keep.tile([P, T], F32, name="rk_pool", align_bytes=64)
+        rk_pool = reuse.tile([P, T], F32, name="rk_pool", offset=2 * N, align_bytes=64)
         nc.vector.memset(rk_pool[:RK_PART, :], 0.0)
         nc.sync.dma_start(rk_pool[RK_PART : RK_PART + 1, :], rk[0:1, :])
 
@@ -96,6 +96,16 @@ def tile_attend_cosexp_topk_kernel(tc, qT, k_words, k_scales, rk, rq, offs, out)
             rk_row = keep.tile([P, last - first], F32, name="rk_row%d" % first, align_bytes=64)
             nc.scalar.activation(rk_row[:], rk_pool[:].indirect(offsets[:, first // 16 : last // 16]), COPY)
             rk_rows.extend(rk_row[:, c : c + P] for c in range(0, last - first, P))
+
+        def cast(copy_call, q_bf, m):
+            copy_call(
+                q_bf[:].rearrange("p (c i) j -> p c j i", i=4),
+                q_raw[:, :, m * P : (m + 1) * P].rearrange("p j (c i) -> p c j i", i=4),
+            )
+
+        second_bf = reuse.tile([P, P, PACK], BF16, name="second_bf", offset=2 * N, align_bytes=64)
+        cast(nc.scalar.copy, second_bf, 1)
+
         for h in range(HALVES):
             turned = psum.tile([P, (BLOCKS, 4 * BANK // (4 * P))[h], P], F32, name="turned%d" % h, offset=BANK * (6, 0)[h])
             for b in range(BLOCKS):
@@ -121,19 +131,18 @@ def tile_attend_cosexp_topk_kernel(tc, qT, k_words, k_scales, rk, rq, offs, out)
             queue = (nc.sync, nc.scalar)[quad % 2]
             queue.dma_start(k_scale[32 * quad : 32 * quad + 4, :], picked_scales[first : first + 4, :].bitcast(I32))
 
-        q_bf = keep.tile([P, NQ, PACK], BF16, name="q_bf", align_bytes=64)
-        nc.vector.tensor_copy(
-            q_bf[:].rearrange("p (c i) j -> p c j i", i=4),
-            q_raw[:].rearrange("p j (c i) -> p c j i", i=4),
-        )
-
         q_codes = keep.tile([P, NQ], U32, name="q_codes", align_bytes=64)
         q_scale = keep.tile([P, NQ], U8, name="q_scale", align_bytes=64)
-        nc.vector.quantize_mx(
-            out=q_codes[:].bitcast(FP8X4),
-            scales=q_scale[:],
-            in_=q_bf[:].rearrange("p n j -> p (n j)"),
-        )
+        first_bf = keep.tile([P, P, PACK], BF16, name="first_bf", align_bytes=64)
+        for m, q_bf in enumerate((first_bf, second_bf)):
+            if m == 0:
+                cast(nc.vector.tensor_copy, q_bf, m)
+            rows = slice(m * P, (m + 1) * P)
+            nc.vector.quantize_mx(
+                out=q_codes[:, rows].bitcast(FP8X4),
+                scales=q_scale[:, rows],
+                in_=q_bf[:].rearrange("p n j -> p (n j)"),
+            )
 
         k_codes = keep.tile([P, N], U32, name="k_codes", align_bytes=64)
         for first in range(0, N, P):

@@ -1,6 +1,7 @@
 from contextlib import ExitStack
 
 import concourse.mybir as mybir
+from concourse.masks import make_identity
 
 D, NQ, N, T = 512, 256, 512, 2048
 FLOPS = 2 * D * NQ * N
@@ -15,7 +16,6 @@ FP8X4 = mybir.dt.float8_e4m3fn_x4
 EXP = mybir.ActivationFunctionType.Exp
 COPY = mybir.ActivationFunctionType.Copy
 MULT = mybir.AluOpType.mult
-NOT_EQUAL = mybir.AluOpType.not_equal
 
 P = 128
 PACK = 4
@@ -27,7 +27,6 @@ RK_PART = P - 1
 SCALE_ROWS = D // 32
 SCALE_PART = 64 - SCALE_ROWS
 BANK = 2048
-LAST_COLS = 16
 
 
 def tile_attend_cosexp_topk_kernel(tc, qT, k_words, k_scales, rk, rq, offs, out):
@@ -37,58 +36,33 @@ def tile_attend_cosexp_topk_kernel(tc, qT, k_words, k_scales, rk, rq, offs, out)
         reuse = ctx.enter_context(tc.tile_pool(name="reuse", bufs=1))
         psum = ctx.enter_context(tc.psum_pool(name="psum", bufs=1))
 
+        rk_pool = reuse.tile([P, T], F32, name="rk_pool", offset=T, align_bytes=64)
+        nc.sync.dma_start(rk_pool[RK_PART : RK_PART + 1, :], rk[0:1, :])
         offsets = keep.tile([P, N // 16], U16, name="offsets")
         nc.sync.dma_start(offsets[:], offs)
+        scale_pool = reuse.tile([P, T // 4], I32, name="scale_pool", offset=0, align_bytes=64)
+        nc.scalar.dma_start(scale_pool[SCALE_PART:64, :], k_scales[0].bitcast(I32))
+        q_raw = keep.tile([P, PACK, NQ], F32, name="q_raw")
+        nc.scalar.dma_start(q_raw[:], qT[0].rearrange("(p j) n -> p j n", j=PACK))
+        word_pool = keep.tile([P, T], I32, name="word_pool", align_bytes=64)
+        nc.sync.dma_start(word_pool[:], k_words[0].rearrange("p t r -> p (t r)").bitcast(I32))
 
         ident = keep.tile([P, P], F32, name="ident")
-
-        def identity_columns(zeros, first, count):
-            nc.gpsimd.affine_select(
-                out=ident[:, first : first + count],
-                in_=zeros,
-                pattern=[[-1, count]],
-                compare_op=NOT_EQUAL,
-                fill=1.0,
-                base=-first,
-                channel_multiplier=1,
-            )
+        make_identity(nc, ident[:])
 
         zero = keep.tile([P, 1], F32, name="zero")
         nc.vector.memset(zero[:], 0.0)
-        wide_zero = reuse.tile([P, P - LAST_COLS], F32, name="wide_zero", offset=8 * LAST_COLS, align_bytes=64)
-        nc.vector.memset(wide_zero[:], 0.0)
-        identity_columns(wide_zero[:], 0, P - LAST_COLS)
-        k_scale = reuse.tile([P, N // 4], I32, name="k_scale", offset=0, align_bytes=64)
-        nc.gpsimd.memset(k_scale[:], 0)
-
-        rk_pool = reuse.tile([P, T], F32, name="rk_pool", offset=2 * N, align_bytes=64)
+        nc.vector.memset(scale_pool[:SCALE_PART, : T // 4 - 1], 0)
+        nc.vector.memset(scale_pool[:SCALE_PART, T // 4 - 1 :], 0)
         nc.vector.memset(rk_pool[:RK_PART, :], 0.0)
-        nc.sync.dma_start(rk_pool[RK_PART : RK_PART + 1, :], rk[0:1, :])
-
-        scale_pool = keep.tile([P, T // 4], I32, name="scale_pool", align_bytes=64)
-        nc.vector.memset(scale_pool[:SCALE_PART, :], 0)
         nc.vector.memset(scale_pool[64:, :], 0)
-        nc.scalar.dma_start(scale_pool[SCALE_PART:64, :], k_scales[0].bitcast(I32))
-
-        q_raw = keep.tile([P, PACK, NQ], F32, name="q_raw")
-        nc.scalar.dma_start(q_raw[:], qT[0].rearrange("(p j) n -> p j n", j=PACK))
-
-        rq_rows = keep.tile([P, P], F32, name="rq_rows")
-        nc.vector.memset(rq_rows[: P - QT, :], 0.0)
-        nc.sync.dma_start(rq_rows[P - QT :, :], rq[0].rearrange("(m p) o -> m (p o)", m=QT))
-
-        word_pool = keep.tile([P, T], I32, name="word_pool", align_bytes=64)
-        nc.sync.dma_start(word_pool[:], k_words[0].rearrange("p t r -> p (t r)").bitcast(I32))
+        k_scale = keep.tile([P, N // 4], I32, name="k_scale", align_bytes=64)
+        nc.vector.memset(k_scale[:], 0)
 
         minus_ten = keep.tile([P, 1], F32, name="minus_ten")
         nc.scalar.activation(minus_ten[:], zero[:], COPY, bias=-10.0)
 
-        last_zero = reuse.tile([P, LAST_COLS], F32, name="last_zero", offset=N, align_bytes=64)
-        nc.gpsimd.memset(last_zero[:], 0.0)
-        identity_columns(last_zero[:], P - LAST_COLS, LAST_COLS)
-
         pieces = ((0, P), (P, NH), (NH, N))
-
         rk_col = keep.tile([P, HALVES, BLOCKS], F32, name="rk_col")
         rk_all = keep.tile([P, N], F32, name="rk_all")
         rk_rows = []
@@ -97,13 +71,17 @@ def tile_attend_cosexp_topk_kernel(tc, qT, k_words, k_scales, rk, rq, offs, out)
             nc.scalar.activation(rk_row[:], rk_pool[:].indirect(offsets[:, first // 16 : last // 16]), COPY)
             rk_rows.extend(rk_row[:, c : c + P] for c in range(0, last - first, P))
 
+        rq_sb = reuse.tile([P, QT], F32, name="rq_sb", offset=3 * T, align_bytes=64)
+        with nc.allow_non_contiguous_dma(reason="one factor a partition"):
+            nc.scalar.dma_start(rq_sb[:], rq[0].rearrange("(m p) o -> p (m o)", m=QT))
+
         def cast(copy_call, q_bf, m):
             copy_call(
                 q_bf[:].rearrange("p (c i) j -> p c j i", i=4),
                 q_raw[:, :, m * P : (m + 1) * P].rearrange("p j (c i) -> p c j i", i=4),
             )
 
-        second_bf = reuse.tile([P, P, PACK], BF16, name="second_bf", offset=2 * N, align_bytes=64)
+        second_bf = reuse.tile([P, P, PACK], BF16, name="second_bf", offset=T, align_bytes=64)
         cast(nc.scalar.copy, second_bf, 1)
 
         for h in range(HALVES):
@@ -111,10 +89,6 @@ def tile_attend_cosexp_topk_kernel(tc, qT, k_words, k_scales, rk, rq, offs, out)
             for b in range(BLOCKS):
                 nc.tensor.transpose(turned[:, b, :], rk_rows[BLOCKS * h + b], ident[:])
             nc.scalar.copy(rk_col[:, h, :], turned[:, :BLOCKS, RK_PART])
-        rq_turned = psum.tile([P, P], F32, name="rq_turned", offset=BANK * 7)
-        nc.tensor.transpose(rq_turned[:], rq_rows[:], ident[:])
-        rq_sb = keep.tile([P, QT], F32, name="rq_sb")
-        nc.scalar.copy(rq_sb[:], rq_turned[:, P - QT :])
 
         for h in range(HALVES):
             for b in range(BLOCKS):
@@ -128,15 +102,13 @@ def tile_attend_cosexp_topk_kernel(tc, qT, k_words, k_scales, rk, rq, offs, out)
         nc.vector.tensor_copy(picked_scales[:], scale_pool[:].bitcast(U8).indirect(offsets[:]))
         for quad in range(4):
             first = SCALE_PART + 4 * quad
-            queue = (nc.sync, nc.scalar)[quad % 2]
-            queue.dma_start(k_scale[32 * quad : 32 * quad + 4, :], picked_scales[first : first + 4, :].bitcast(I32))
+            nc.sync.dma_start(k_scale[32 * quad : 32 * quad + 4, :], picked_scales[first : first + 4, :].bitcast(I32))
 
         q_codes = keep.tile([P, NQ], U32, name="q_codes", align_bytes=64)
         q_scale = keep.tile([P, NQ], U8, name="q_scale", align_bytes=64)
-        first_bf = keep.tile([P, P, PACK], BF16, name="first_bf", align_bytes=64)
+        first_bf = reuse.tile([P, P, PACK], BF16, name="first_bf", offset=0, align_bytes=64)
+        cast(nc.vector.tensor_copy, first_bf, 0)
         for m, q_bf in enumerate((first_bf, second_bf)):
-            if m == 0:
-                cast(nc.vector.tensor_copy, q_bf, m)
             rows = slice(m * P, (m + 1) * P)
             nc.vector.quantize_mx(
                 out=q_codes[:, rows].bitcast(FP8X4),
@@ -144,7 +116,7 @@ def tile_attend_cosexp_topk_kernel(tc, qT, k_words, k_scales, rk, rq, offs, out)
                 in_=q_bf[:].rearrange("p n j -> p (n j)"),
             )
 
-        k_codes = keep.tile([P, N], U32, name="k_codes", align_bytes=64)
+        k_codes = reuse.tile([P, N], U32, name="k_codes", offset=T, align_bytes=64)
         for first in range(0, N, P):
             nc.vector.tensor_copy(
                 k_codes[:, first : first + P],

@@ -36,10 +36,12 @@ def tile_attend_cosexp_topk_kernel(tc, qT, k_words, k_scales, rk, rq, offs, out)
         reuse = ctx.enter_context(tc.tile_pool(name="reuse", bufs=1))
         psum = ctx.enter_context(tc.psum_pool(name="psum", bufs=1))
 
-        rk_pool = reuse.tile([P, T], F32, name="rk_pool", offset=T, align_bytes=64)
-        nc.sync.dma_start(rk_pool[RK_PART : RK_PART + 1, :], rk[0:1, :])
         offsets = keep.tile([P, N // 16], U16, name="offsets")
         nc.sync.dma_start(offsets[:], offs)
+        rk_pool = reuse.tile([P, T], F32, name="rk_pool", offset=T, align_bytes=64)
+        nc.sync.dma_start(rk_pool[RK_PART : RK_PART + 1, :], rk[0:1, :])
+        rq_rows = keep.tile([P, P], F32, name="rq_rows")
+        nc.sync.dma_start(rq_rows[P - QT :, :], rq[0].rearrange("(m p) o -> m (p o)", m=QT))
         scale_pool = reuse.tile([P, T // 4], I32, name="scale_pool", offset=0, align_bytes=64)
         nc.scalar.dma_start(scale_pool[SCALE_PART:64, :], k_scales[0].bitcast(I32))
         q_raw = keep.tile([P, PACK, NQ], F32, name="q_raw")
@@ -58,6 +60,7 @@ def tile_attend_cosexp_topk_kernel(tc, qT, k_words, k_scales, rk, rq, offs, out)
         nc.vector.memset(scale_pool[64:, :], 0)
         k_scale = keep.tile([P, N // 4], I32, name="k_scale", align_bytes=64)
         nc.vector.memset(k_scale[:], 0)
+        nc.vector.memset(rq_rows[: P - QT, :], 0.0)
 
         minus_ten = keep.tile([P, 1], F32, name="minus_ten")
         nc.scalar.activation(minus_ten[:], zero[:], COPY, bias=-10.0)
@@ -70,10 +73,6 @@ def tile_attend_cosexp_topk_kernel(tc, qT, k_words, k_scales, rk, rq, offs, out)
             rk_row = keep.tile([P, last - first], F32, name="rk_row%d" % first, align_bytes=64)
             nc.scalar.activation(rk_row[:], rk_pool[:].indirect(offsets[:, first // 16 : last // 16]), COPY)
             rk_rows.extend(rk_row[:, c : c + P] for c in range(0, last - first, P))
-
-        rq_sb = reuse.tile([P, QT], F32, name="rq_sb", offset=3 * T, align_bytes=64)
-        with nc.allow_non_contiguous_dma(reason="one factor a partition"):
-            nc.scalar.dma_start(rq_sb[:], rq[0].rearrange("(m p) o -> p (m o)", m=QT))
 
         def cast(copy_call, q_bf, m):
             copy_call(
@@ -89,6 +88,10 @@ def tile_attend_cosexp_topk_kernel(tc, qT, k_words, k_scales, rk, rq, offs, out)
             for b in range(BLOCKS):
                 nc.tensor.transpose(turned[:, b, :], rk_rows[BLOCKS * h + b], ident[:])
             nc.scalar.copy(rk_col[:, h, :], turned[:, :BLOCKS, RK_PART])
+        rq_turned = psum.tile([P, P], F32, name="rq_turned", offset=BANK * 7)
+        nc.tensor.transpose(rq_turned[:], rq_rows[:], ident[:])
+        rq_sb = keep.tile([P, QT], F32, name="rq_sb")
+        nc.scalar.copy(rq_sb[:], rq_turned[:, P - QT :])
 
         for h in range(HALVES):
             for b in range(BLOCKS):
@@ -106,7 +109,7 @@ def tile_attend_cosexp_topk_kernel(tc, qT, k_words, k_scales, rk, rq, offs, out)
 
         q_codes = keep.tile([P, NQ], U32, name="q_codes", align_bytes=64)
         q_scale = keep.tile([P, NQ], U8, name="q_scale", align_bytes=64)
-        first_bf = reuse.tile([P, P, PACK], BF16, name="first_bf", offset=0, align_bytes=64)
+        first_bf = keep.tile([P, P, PACK], BF16, name="first_bf", align_bytes=64)
         cast(nc.vector.tensor_copy, first_bf, 0)
         for m, q_bf in enumerate((first_bf, second_bf)):
             rows = slice(m * P, (m + 1) * P)

@@ -1,7 +1,6 @@
 from contextlib import ExitStack
 
 import concourse.mybir as mybir
-from concourse.masks import make_identity
 
 D, NQ, N, T = 512, 256, 512, 2048
 FLOPS = 2 * D * NQ * N
@@ -16,6 +15,7 @@ FP8X4 = mybir.dt.float8_e4m3fn_x4
 EXP = mybir.ActivationFunctionType.Exp
 COPY = mybir.ActivationFunctionType.Copy
 MULT = mybir.AluOpType.mult
+NOT_EQUAL = mybir.AluOpType.not_equal
 
 P = 128
 PACK = 4
@@ -38,25 +38,33 @@ def tile_attend_cosexp_topk_kernel(tc, qT, k_words, k_scales, rk, rq, offs, out)
 
         offsets = keep.tile([P, N // 16], U16, name="offsets")
         nc.sync.dma_start(offsets[:], offs)
-        rk_pool = reuse.tile([P, T], F32, name="rk_pool", offset=T, align_bytes=64)
+        rk_pool = keep.tile([P, T], F32, name="rk_pool", align_bytes=64)
         nc.sync.dma_start(rk_pool[RK_PART : RK_PART + 1, :], rk[0:1, :])
         rq_rows = keep.tile([P, P], F32, name="rq_rows")
         nc.sync.dma_start(rq_rows[P - QT :, :], rq[0].rearrange("(m p) o -> m (p o)", m=QT))
-        scale_pool = reuse.tile([P, T // 4], I32, name="scale_pool", offset=0, align_bytes=64)
+        scale_pool = keep.tile([P, T // 4], I32, name="scale_pool", align_bytes=64)
         nc.scalar.dma_start(scale_pool[SCALE_PART:64, :], k_scales[0].bitcast(I32))
         q_raw = keep.tile([P, PACK, NQ], F32, name="q_raw")
         nc.scalar.dma_start(q_raw[:], qT[0].rearrange("(p j) n -> p j n", j=PACK))
         word_pool = keep.tile([P, T], I32, name="word_pool", align_bytes=64)
         nc.sync.dma_start(word_pool[:], k_words[0].rearrange("p t r -> p (t r)").bitcast(I32))
 
-        ident = keep.tile([P, P], F32, name="ident")
-        make_identity(nc, ident[:])
-
         zero = keep.tile([P, 1], F32, name="zero")
         nc.vector.memset(zero[:], 0.0)
-        nc.vector.memset(scale_pool[:SCALE_PART, : T // 4 - 1], 0)
-        nc.vector.memset(scale_pool[:SCALE_PART, T // 4 - 1 :], 0)
+        square_zero = keep.tile([P, P], F32, name="square_zero")
+        nc.vector.memset(square_zero[:], 0.0)
+        ident = keep.tile([P, P], F32, name="ident")
+        nc.gpsimd.affine_select(
+            out=ident[:],
+            in_=square_zero[:],
+            pattern=[[-1, P]],
+            compare_op=NOT_EQUAL,
+            fill=1.0,
+            base=0,
+            channel_multiplier=1,
+        )
         nc.vector.memset(rk_pool[:RK_PART, :], 0.0)
+        nc.vector.memset(scale_pool[:SCALE_PART, :], 0)
         nc.vector.memset(scale_pool[64:, :], 0)
         k_scale = keep.tile([P, N // 4], I32, name="k_scale", align_bytes=64)
         nc.vector.memset(k_scale[:], 0)
@@ -70,7 +78,7 @@ def tile_attend_cosexp_topk_kernel(tc, qT, k_words, k_scales, rk, rq, offs, out)
         rk_all = keep.tile([P, N], F32, name="rk_all")
         rk_rows = []
         for first, last in pieces:
-            rk_row = keep.tile([P, last - first], F32, name="rk_row%d" % first, align_bytes=64)
+            rk_row = reuse.tile([P, last - first], F32, name="rk_row%d" % first, offset=8 * first, align_bytes=64)
             nc.scalar.activation(rk_row[:], rk_pool[:].indirect(offsets[:, first // 16 : last // 16]), COPY)
             rk_rows.extend(rk_row[:, c : c + P] for c in range(0, last - first, P))
 
@@ -80,14 +88,14 @@ def tile_attend_cosexp_topk_kernel(tc, qT, k_words, k_scales, rk, rq, offs, out)
                 q_raw[:, :, m * P : (m + 1) * P].rearrange("p j (c i) -> p c j i", i=4),
             )
 
-        second_bf = reuse.tile([P, P, PACK], BF16, name="second_bf", offset=T, align_bytes=64)
-        cast(nc.scalar.copy, second_bf, 1)
-
+        second_bf = reuse.tile([P, P, PACK], BF16, name="second_bf", offset=8 * P, align_bytes=64)
         for h in range(HALVES):
             turned = psum.tile([P, (BLOCKS, 4 * BANK // (4 * P))[h], P], F32, name="turned%d" % h, offset=BANK * (6, 0)[h])
             for b in range(BLOCKS):
                 nc.tensor.transpose(turned[:, b, :], rk_rows[BLOCKS * h + b], ident[:])
             nc.scalar.copy(rk_col[:, h, :], turned[:, :BLOCKS, RK_PART])
+            if h == 0:
+                cast(nc.scalar.copy, second_bf, 1)
         rq_turned = psum.tile([P, P], F32, name="rq_turned", offset=BANK * 7)
         nc.tensor.transpose(rq_turned[:], rq_rows[:], ident[:])
         rq_sb = keep.tile([P, QT], F32, name="rq_sb")
@@ -119,7 +127,7 @@ def tile_attend_cosexp_topk_kernel(tc, qT, k_words, k_scales, rk, rq, offs, out)
                 in_=q_bf[:].rearrange("p n j -> p (n j)"),
             )
 
-        k_codes = reuse.tile([P, N], U32, name="k_codes", offset=T, align_bytes=64)
+        k_codes = reuse.tile([P, N], U32, name="k_codes", offset=0, align_bytes=64)
         for first in range(0, N, P):
             nc.vector.tensor_copy(
                 k_codes[:, first : first + P],

@@ -38,7 +38,7 @@ def tile_attend_cosexp_topk_kernel(tc, qT, k_words, k_scales, rk, rq, offs, out)
 
         offsets = keep.tile([P, N // 16], U16, name="offsets")
         nc.sync.dma_start(offsets[:], offs)
-        rk_pool = keep.tile([P, T], F32, name="rk_pool", align_bytes=64)
+        rk_pool = reuse.tile([P, T], F32, name="rk_pool", offset=0, align_bytes=64)
         nc.sync.dma_start(rk_pool[RK_PART : RK_PART + 1, :], rk[0:1, :])
         rq_rows = keep.tile([P, P], F32, name="rq_rows")
         nc.sync.dma_start(rq_rows[P - QT :, :], rq[0].rearrange("(m p) o -> m (p o)", m=QT))
@@ -72,13 +72,15 @@ def tile_attend_cosexp_topk_kernel(tc, qT, k_words, k_scales, rk, rq, offs, out)
 
         minus_ten = keep.tile([P, 1], F32, name="minus_ten")
         nc.scalar.activation(minus_ten[:], zero[:], COPY, bias=-10.0)
+        ten = reuse.tile([P, 1], F32, name="ten", offset=4 * T, align_bytes=64)
+        nc.scalar.activation(ten[:], zero[:], COPY, bias=10.0)
 
         pieces = ((0, P), (P, NH), (NH, N))
         rk_col = keep.tile([P, HALVES, BLOCKS], F32, name="rk_col")
         rk_all = keep.tile([P, N], F32, name="rk_all")
         rk_rows = []
         for first, last in pieces:
-            rk_row = reuse.tile([P, last - first], F32, name="rk_row%d" % first, offset=8 * first, align_bytes=64)
+            rk_row = keep.tile([P, last - first], F32, name="rk_row%d" % first, align_bytes=64)
             nc.scalar.activation(rk_row[:], rk_pool[:].indirect(offsets[:, first // 16 : last // 16]), COPY)
             rk_rows.extend(rk_row[:, c : c + P] for c in range(0, last - first, P))
 
@@ -88,15 +90,14 @@ def tile_attend_cosexp_topk_kernel(tc, qT, k_words, k_scales, rk, rq, offs, out)
                 q_raw[:, :, m * P : (m + 1) * P].rearrange("p j (c i) -> p c j i", i=4),
             )
 
-        second_bf = reuse.tile([P, P, PACK], BF16, name="second_bf", offset=8 * P, align_bytes=64)
+        second_bf = reuse.tile([P, P, PACK], BF16, name="second_bf", offset=0, align_bytes=64)
+        cast(nc.scalar.copy, second_bf, 1)
         for h in range(HALVES):
-            turned = psum.tile([P, (BLOCKS, 4 * BANK // (4 * P))[h], P], F32, name="turned%d" % h, offset=BANK * (6, 0)[h])
+            turned = psum.tile([P, BLOCKS, P], F32, name="turned%d" % h, offset=BANK * (6 + h))
             for b in range(BLOCKS):
                 nc.tensor.transpose(turned[:, b, :], rk_rows[BLOCKS * h + b], ident[:])
-            nc.scalar.copy(rk_col[:, h, :], turned[:, :BLOCKS, RK_PART])
-            if h == 0:
-                cast(nc.scalar.copy, second_bf, 1)
-        rq_turned = psum.tile([P, P], F32, name="rq_turned", offset=BANK * 7)
+            nc.scalar.copy(rk_col[:, h, :], turned[:, :, RK_PART])
+        rq_turned = psum.tile([P, P], F32, name="rq_turned", offset=BANK * 5)
         nc.tensor.transpose(rq_turned[:], rq_rows[:], ident[:])
         rq_sb = keep.tile([P, QT], F32, name="rq_sb")
         nc.scalar.copy(rq_sb[:], rq_turned[:, P - QT :])
@@ -107,7 +108,7 @@ def tile_attend_cosexp_topk_kernel(tc, qT, k_words, k_scales, rk, rq, offs, out)
                 block = BLOCKS * h + b
                 spread = psum.tile([P, P], F32, name="spread%d" % block, offset=BANK * (4 + block))
                 nc.tensor.transpose(spread[:], rk_col[:, h, b : b + 1].to_broadcast([P, P]), ident[:])
-                nc.scalar.activation(rk_all[:, first : first + P], spread[:], COPY, scale=10.0)
+                nc.scalar.activation(rk_all[:, first : first + P], spread[:], COPY, scale=(ten[:], 10.0)[h])
 
         picked_scales = keep.tile([P, N], U8, name="picked_scales", align_bytes=64)
         nc.vector.tensor_copy(picked_scales[:], scale_pool[:].bitcast(U8).indirect(offsets[:]))
@@ -127,12 +128,13 @@ def tile_attend_cosexp_topk_kernel(tc, qT, k_words, k_scales, rk, rq, offs, out)
                 in_=q_bf[:].rearrange("p n j -> p (n j)"),
             )
 
-        k_codes = reuse.tile([P, N], U32, name="k_codes", offset=0, align_bytes=64)
+        k_codes = []
         for first in range(0, N, P):
+            codes = reuse.tile([P, P], U32, name="k_codes%d" % first, offset=4 * (T + N - P - first), align_bytes=64)
             nc.vector.tensor_copy(
-                k_codes[:, first : first + P],
-                word_pool[:].bitcast(U32).indirect(offsets[:, first // 16 : (first + P) // 16]),
+                codes[:], word_pool[:].bitcast(U32).indirect(offsets[:, first // 16 : (first + P) // 16])
             )
+            k_codes.append(codes)
 
         out_by_tile = out[0].rearrange("(m p) n -> p m n", m=QT)
         for block in range(N // P):
@@ -141,12 +143,12 @@ def tile_attend_cosexp_topk_kernel(tc, qT, k_words, k_scales, rk, rq, offs, out)
             for m in range(QT):
                 rows = slice(m * P, (m + 1) * P)
                 step = block * QT + m
-                acc = psum.tile([P, P], F32, name="acc%d" % step, offset=BANK * step)
+                acc = psum.tile([P, P], F32, name="acc%d" % step, offset=BANK * (block, 4 + (0, 2, 3, 1)[block])[m])
                 nc.tensor.matmul_mx(
                     out=acc[:],
                     lhsT=q_codes[:, rows].bitcast(FP8X4),
                     lhsT_scale=q_scale[:, rows],
-                    rhs=k_codes[:, slots].bitcast(FP8X4),
+                    rhs=k_codes[block][:].bitcast(FP8X4),
                     rhs_scale=k_scale[:].bitcast(U8)[:, slots],
                     start=True,
                     stop=True,

@@ -27,6 +27,7 @@ RK_PART = P - 1
 SCALE_ROWS = D // 32
 SCALE_PART = 64 - SCALE_ROWS
 BANK = 2048
+FIRST = 4 * (T + N)
 
 
 def tile_attend_cosexp_topk_kernel(tc, qT, k_words, k_scales, rk, rq, offs, out):
@@ -49,9 +50,9 @@ def tile_attend_cosexp_topk_kernel(tc, qT, k_words, k_scales, rk, rq, offs, out)
         word_pool = keep.tile([P, T], I32, name="word_pool", align_bytes=64)
         nc.sync.dma_start(word_pool[:], k_words[0].rearrange("p t r -> p (t r)").bitcast(I32))
 
-        zero = keep.tile([P, 1], F32, name="zero")
+        zero = reuse.tile([P, 1], F32, name="zero", offset=FIRST, align_bytes=64)
         nc.vector.memset(zero[:], 0.0)
-        square_zero = keep.tile([P, P], F32, name="square_zero")
+        square_zero = reuse.tile([P, P], F32, name="square_zero", offset=FIRST + 64, align_bytes=64)
         nc.vector.memset(square_zero[:], 0.0)
         ident = keep.tile([P, P], F32, name="ident")
         nc.gpsimd.affine_select(
@@ -66,14 +67,15 @@ def tile_attend_cosexp_topk_kernel(tc, qT, k_words, k_scales, rk, rq, offs, out)
         nc.vector.memset(rk_pool[:RK_PART, :], 0.0)
         nc.vector.memset(scale_pool[:SCALE_PART, :], 0)
         nc.vector.memset(scale_pool[64:, :], 0)
-        k_scale = keep.tile([P, N // 4], I32, name="k_scale", align_bytes=64)
-        nc.vector.memset(k_scale[:], 0)
         nc.vector.memset(rq_rows[: P - QT, :], 0.0)
 
         minus_ten = keep.tile([P, 1], F32, name="minus_ten")
         nc.scalar.activation(minus_ten[:], zero[:], COPY, bias=-10.0)
         ten = reuse.tile([P, 1], F32, name="ten", offset=4 * T, align_bytes=64)
         nc.scalar.activation(ten[:], zero[:], COPY, bias=10.0)
+
+        k_scale = reuse.tile([P, N // 4], I32, name="k_scale", offset=FIRST, align_bytes=64)
+        nc.gpsimd.memset(k_scale[:], 0)
 
         pieces = ((0, P), (P, NH), (NH, N))
         rk_col = keep.tile([P, HALVES, BLOCKS], F32, name="rk_col")
@@ -92,6 +94,13 @@ def tile_attend_cosexp_topk_kernel(tc, qT, k_words, k_scales, rk, rq, offs, out)
 
         second_bf = reuse.tile([P, P, PACK], BF16, name="second_bf", offset=0, align_bytes=64)
         cast(nc.scalar.copy, second_bf, 1)
+        picked_scales = keep.tile([P, N], U8, name="picked_scales", align_bytes=64)
+        nc.vector.tensor_copy(picked_scales[:], scale_pool[:].bitcast(U8).indirect(offsets[:]))
+        for quad in range(4):
+            first = SCALE_PART + 4 * quad
+            queue = (nc.sync, nc.scalar)[quad % 2]
+            queue.dma_start(k_scale[32 * quad : 32 * quad + 4, :], picked_scales[first : first + 4, :].bitcast(I32))
+
         for h in range(HALVES):
             turned = psum.tile([P, BLOCKS, P], F32, name="turned%d" % h, offset=BANK * (6 + h))
             for b in range(BLOCKS):
@@ -109,12 +118,6 @@ def tile_attend_cosexp_topk_kernel(tc, qT, k_words, k_scales, rk, rq, offs, out)
                 spread = psum.tile([P, P], F32, name="spread%d" % block, offset=BANK * (4 + block))
                 nc.tensor.transpose(spread[:], rk_col[:, h, b : b + 1].to_broadcast([P, P]), ident[:])
                 nc.scalar.activation(rk_all[:, first : first + P], spread[:], COPY, scale=(ten[:], 10.0)[h])
-
-        picked_scales = keep.tile([P, N], U8, name="picked_scales", align_bytes=64)
-        nc.vector.tensor_copy(picked_scales[:], scale_pool[:].bitcast(U8).indirect(offsets[:]))
-        for quad in range(4):
-            first = SCALE_PART + 4 * quad
-            nc.sync.dma_start(k_scale[32 * quad : 32 * quad + 4, :], picked_scales[first : first + 4, :].bitcast(I32))
 
         q_codes = keep.tile([P, NQ], U32, name="q_codes", align_bytes=64)
         q_scale = keep.tile([P, NQ], U8, name="q_scale", align_bytes=64)

@@ -27,6 +27,7 @@ RK_PART = P - 1
 SCALE_ROWS = D // 32
 SCALE_PART = 64 - SCALE_ROWS
 BANK = 2048
+LAST_ROWS = 64
 FIRST = 4 * (T + N)
 
 
@@ -86,14 +87,15 @@ def tile_attend_cosexp_topk_kernel(tc, qT, k_words, k_scales, rk, rq, offs, out)
             nc.scalar.activation(rk_row[:], rk_pool[:].indirect(offsets[:, first // 16 : last // 16]), COPY)
             rk_rows.extend(rk_row[:, c : c + P] for c in range(0, last - first, P))
 
-        def cast(copy_call, q_bf, m):
+        def cast(copy_call, q_bf, rows):
             copy_call(
                 q_bf[:].rearrange("p (c i) j -> p c j i", i=4),
-                q_raw[:, :, m * P : (m + 1) * P].rearrange("p j (c i) -> p c j i", i=4),
+                q_raw[:, :, rows].rearrange("p j (c i) -> p c j i", i=4),
             )
 
-        second_bf = reuse.tile([P, P, PACK], BF16, name="second_bf", offset=0, align_bytes=64)
-        cast(nc.scalar.copy, second_bf, 1)
+        q_parts = (slice(0, P), slice(P, NQ - LAST_ROWS), slice(NQ - LAST_ROWS, NQ))
+        last_bf = reuse.tile([P, LAST_ROWS, PACK], BF16, name="last_bf", offset=0, align_bytes=64)
+        cast(nc.scalar.copy, last_bf, q_parts[2])
         picked_scales = keep.tile([P, N], U8, name="picked_scales", align_bytes=64)
         nc.vector.tensor_copy(picked_scales[:], scale_pool[:].bitcast(U8).indirect(offsets[:]))
         for quad in range(4):
@@ -122,9 +124,10 @@ def tile_attend_cosexp_topk_kernel(tc, qT, k_words, k_scales, rk, rq, offs, out)
         q_codes = keep.tile([P, NQ], U32, name="q_codes", align_bytes=64)
         q_scale = keep.tile([P, NQ], U8, name="q_scale", align_bytes=64)
         first_bf = keep.tile([P, P, PACK], BF16, name="first_bf", align_bytes=64)
-        cast(nc.vector.tensor_copy, first_bf, 0)
-        for m, q_bf in enumerate((first_bf, second_bf)):
-            rows = slice(m * P, (m + 1) * P)
+        cast(nc.vector.tensor_copy, first_bf, q_parts[0])
+        second_bf = keep.tile([P, P - LAST_ROWS, PACK], BF16, name="second_bf", align_bytes=64)
+        cast(nc.vector.tensor_copy, second_bf, q_parts[1])
+        for rows, q_bf in zip(q_parts, (first_bf, second_bf, last_bf)):
             nc.vector.quantize_mx(
                 out=q_codes[:, rows].bitcast(FP8X4),
                 scales=q_scale[:, rows],

@@ -29,6 +29,7 @@ SCALE_PART = 64 - SCALE_ROWS
 BANK = 2048
 LAST_ROWS = 64
 FIRST = 4 * (T + N)
+SECOND = FIRST + 1024
 
 
 def tile_attend_cosexp_topk_kernel(tc, qT, k_words, k_scales, rk, rq, offs, out):
@@ -42,8 +43,6 @@ def tile_attend_cosexp_topk_kernel(tc, qT, k_words, k_scales, rk, rq, offs, out)
         nc.sync.dma_start(offsets[:], offs)
         rk_pool = reuse.tile([P, T], F32, name="rk_pool", offset=0, align_bytes=64)
         nc.sync.dma_start(rk_pool[RK_PART : RK_PART + 1, :], rk[0:1, :])
-        rq_rows = keep.tile([P, P], F32, name="rq_rows")
-        nc.sync.dma_start(rq_rows[P - QT :, :], rq[0].rearrange("(m p) o -> m (p o)", m=QT))
         scale_pool = keep.tile([P, T // 4], I32, name="scale_pool", align_bytes=64)
         nc.scalar.dma_start(scale_pool[SCALE_PART:64, :], k_scales[0].bitcast(I32))
         q_raw = keep.tile([P, PACK, NQ], F32, name="q_raw")
@@ -68,7 +67,6 @@ def tile_attend_cosexp_topk_kernel(tc, qT, k_words, k_scales, rk, rq, offs, out)
         nc.vector.memset(rk_pool[:RK_PART, :], 0.0)
         nc.vector.memset(scale_pool[:SCALE_PART, :], 0)
         nc.vector.memset(scale_pool[64:, :], 0)
-        nc.vector.memset(rq_rows[: P - QT, :], 0.0)
 
         minus_ten = keep.tile([P, 1], F32, name="minus_ten")
         nc.scalar.activation(minus_ten[:], zero[:], COPY, bias=-10.0)
@@ -83,7 +81,7 @@ def tile_attend_cosexp_topk_kernel(tc, qT, k_words, k_scales, rk, rq, offs, out)
         rk_all = keep.tile([P, N], F32, name="rk_all")
         rk_rows = []
         for first, last in pieces:
-            rk_row = keep.tile([P, last - first], F32, name="rk_row%d" % first, align_bytes=64)
+            rk_row = reuse.tile([P, last - first], F32, name="rk_row%d" % first, offset=SECOND + 4 * first, align_bytes=64)
             nc.scalar.activation(rk_row[:], rk_pool[:].indirect(offsets[:, first // 16 : last // 16]), COPY)
             rk_rows.extend(rk_row[:, c : c + P] for c in range(0, last - first, P))
 
@@ -100,18 +98,18 @@ def tile_attend_cosexp_topk_kernel(tc, qT, k_words, k_scales, rk, rq, offs, out)
         nc.vector.tensor_copy(picked_scales[:], scale_pool[:].bitcast(U8).indirect(offsets[:]))
         for quad in range(4):
             first = SCALE_PART + 4 * quad
-            queue = (nc.sync, nc.scalar)[quad % 2]
+            queue = (nc.scalar, nc.sync)[quad % 2]
             queue.dma_start(k_scale[32 * quad : 32 * quad + 4, :], picked_scales[first : first + 4, :].bitcast(I32))
 
+        rq_sb = reuse.tile([P, QT], F32, name="rq_sb", offset=SECOND + 4 * P, align_bytes=64)
         for h in range(HALVES):
             turned = psum.tile([P, BLOCKS, P], F32, name="turned%d" % h, offset=BANK * (6 + h))
             for b in range(BLOCKS):
                 nc.tensor.transpose(turned[:, b, :], rk_rows[BLOCKS * h + b], ident[:])
+            if h == 0:
+                with nc.allow_non_contiguous_dma(reason="one factor a partition"):
+                    nc.scalar.dma_start(rq_sb[:], rq[0].rearrange("(m p) o -> p (m o)", m=QT))
             nc.scalar.copy(rk_col[:, h, :], turned[:, :, RK_PART])
-        rq_turned = psum.tile([P, P], F32, name="rq_turned", offset=BANK * 5)
-        nc.tensor.transpose(rq_turned[:], rq_rows[:], ident[:])
-        rq_sb = keep.tile([P, QT], F32, name="rq_sb")
-        nc.scalar.copy(rq_sb[:], rq_turned[:, P - QT :])
 
         for h in range(HALVES):
             for b in range(BLOCKS):

@@ -27,8 +27,7 @@ RK_PART = P - 1
 SCALE_ROWS = D // 32
 SCALE_PART = 64 - SCALE_ROWS
 BANK = 2048
-LAST_ROWS = 64
-FIRST = 4 * (T + N)
+FIRST = 4 * N
 SECOND = FIRST + 1024
 
 
@@ -41,7 +40,7 @@ def tile_attend_cosexp_topk_kernel(tc, qT, k_words, k_scales, rk, rq, offs, out)
 
         offsets = keep.tile([P, N // 16], U16, name="offsets")
         nc.sync.dma_start(offsets[:], offs)
-        rk_pool = reuse.tile([P, T], F32, name="rk_pool", offset=0, align_bytes=64)
+        rk_pool = keep.tile([P, T], F32, name="rk_pool", align_bytes=64)
         nc.sync.dma_start(rk_pool[RK_PART : RK_PART + 1, :], rk[0:1, :])
         scale_pool = keep.tile([P, T // 4], I32, name="scale_pool", align_bytes=64)
         nc.scalar.dma_start(scale_pool[SCALE_PART:64, :], k_scales[0].bitcast(I32))
@@ -70,14 +69,14 @@ def tile_attend_cosexp_topk_kernel(tc, qT, k_words, k_scales, rk, rq, offs, out)
 
         minus_ten = keep.tile([P, 1], F32, name="minus_ten")
         nc.scalar.activation(minus_ten[:], zero[:], COPY, bias=-10.0)
-        ten = reuse.tile([P, 1], F32, name="ten", offset=4 * T, align_bytes=64)
+        ten = reuse.tile([P, 1], F32, name="ten", offset=0, align_bytes=64)
         nc.scalar.activation(ten[:], zero[:], COPY, bias=10.0)
 
         k_scale = reuse.tile([P, N // 4], I32, name="k_scale", offset=FIRST, align_bytes=64)
         nc.gpsimd.memset(k_scale[:], 0)
 
-        pieces = ((0, P), (P, NH), (NH, N))
-        rk_col = keep.tile([P, HALVES, BLOCKS], F32, name="rk_col")
+        pieces = ((0, NH), (NH, NH + P), (NH + P, N))
+        rk_col = keep.tile([P, N // P], F32, name="rk_col")
         rk_all = keep.tile([P, N], F32, name="rk_all")
         rk_rows = []
         for first, last in pieces:
@@ -85,15 +84,6 @@ def tile_attend_cosexp_topk_kernel(tc, qT, k_words, k_scales, rk, rq, offs, out)
             nc.scalar.activation(rk_row[:], rk_pool[:].indirect(offsets[:, first // 16 : last // 16]), COPY)
             rk_rows.extend(rk_row[:, c : c + P] for c in range(0, last - first, P))
 
-        def cast(copy_call, q_bf, rows):
-            copy_call(
-                q_bf[:].rearrange("p (c i) j -> p c j i", i=4),
-                q_raw[:, :, rows].rearrange("p j (c i) -> p c j i", i=4),
-            )
-
-        q_parts = (slice(0, P), slice(P, NQ - LAST_ROWS), slice(NQ - LAST_ROWS, NQ))
-        last_bf = reuse.tile([P, LAST_ROWS, PACK], BF16, name="last_bf", offset=0, align_bytes=64)
-        cast(nc.scalar.copy, last_bf, q_parts[2])
         picked_scales = keep.tile([P, N], U8, name="picked_scales", align_bytes=64)
         nc.vector.tensor_copy(picked_scales[:], scale_pool[:].bitcast(U8).indirect(offsets[:]))
         for quad in range(4):
@@ -101,40 +91,44 @@ def tile_attend_cosexp_topk_kernel(tc, qT, k_words, k_scales, rk, rq, offs, out)
             queue = (nc.scalar, nc.sync)[quad % 2]
             queue.dma_start(k_scale[32 * quad : 32 * quad + 4, :], picked_scales[first : first + 4, :].bitcast(I32))
 
-        rq_sb = reuse.tile([P, QT], F32, name="rq_sb", offset=SECOND + 4 * P, align_bytes=64)
-        for h in range(HALVES):
-            turned = psum.tile([P, BLOCKS, P], F32, name="turned%d" % h, offset=BANK * (6 + h))
-            for b in range(BLOCKS):
-                nc.tensor.transpose(turned[:, b, :], rk_rows[BLOCKS * h + b], ident[:])
-            if h == 0:
-                with nc.allow_non_contiguous_dma(reason="one factor a partition"):
-                    nc.scalar.dma_start(rq_sb[:], rq[0].rearrange("(m p) o -> p (m o)", m=QT))
-            nc.scalar.copy(rk_col[:, h, :], turned[:, :, RK_PART])
+        for piece, (first, last) in enumerate(pieces):
+            blocks = range(first // P, last // P)
+            turned = psum.tile([P, len(blocks), P], F32, name="turned%d" % piece, offset=BANK * (5 + piece))
+            for b, block in enumerate(blocks):
+                nc.tensor.transpose(turned[:, b, :], rk_rows[block], ident[:])
+            nc.scalar.copy(rk_col[:, blocks.start : blocks.stop], turned[:, :, RK_PART])
 
-        for h in range(HALVES):
-            for b in range(BLOCKS):
-                first = h * NH + b * P
-                block = BLOCKS * h + b
-                spread = psum.tile([P, P], F32, name="spread%d" % block, offset=BANK * (4 + block))
-                nc.tensor.transpose(spread[:], rk_col[:, h, b : b + 1].to_broadcast([P, P]), ident[:])
-                nc.scalar.activation(rk_all[:, first : first + P], spread[:], COPY, scale=(ten[:], 10.0)[h])
+        rq_sb = reuse.tile([P, QT], F32, name="rq_sb", offset=SECOND, align_bytes=64)
+        with nc.allow_non_contiguous_dma(reason="one factor a partition"):
+            nc.sync.dma_start(rq_sb[:], rq[0].rearrange("(m p) o -> p (m o)", m=QT))
+
+        for block in range(N // P):
+            spread = psum.tile([P, P], F32, name="spread%d" % block, offset=BANK * (4 + block))
+            nc.tensor.transpose(spread[:], rk_col[:, block : block + 1].to_broadcast([P, P]), ident[:])
+            nc.scalar.activation(
+                rk_all[:, block * P : (block + 1) * P], spread[:], COPY, scale=ten[:] if block < BLOCKS else 10.0
+            )
 
         q_codes = keep.tile([P, NQ], U32, name="q_codes", align_bytes=64)
         q_scale = keep.tile([P, NQ], U8, name="q_scale", align_bytes=64)
-        first_bf = keep.tile([P, P, PACK], BF16, name="first_bf", align_bytes=64)
-        cast(nc.vector.tensor_copy, first_bf, q_parts[0])
-        second_bf = keep.tile([P, P - LAST_ROWS, PACK], BF16, name="second_bf", align_bytes=64)
-        cast(nc.vector.tensor_copy, second_bf, q_parts[1])
-        for rows, q_bf in zip(q_parts, (first_bf, second_bf, last_bf)):
+        q_bf = keep.tile([P, NQ, PACK], BF16, name="q_bf", align_bytes=64)
+        for m in range(QT):
+            rows = slice(m * P, (m + 1) * P)
+            nc.vector.tensor_copy(
+                q_bf[:, rows, :].rearrange("p (c i) j -> p c j i", i=4),
+                q_raw[:, :, rows].rearrange("p j (c i) -> p c j i", i=4),
+            )
+        for m in range(QT):
+            rows = slice(m * P, (m + 1) * P)
             nc.vector.quantize_mx(
                 out=q_codes[:, rows].bitcast(FP8X4),
                 scales=q_scale[:, rows],
-                in_=q_bf[:].rearrange("p n j -> p (n j)"),
+                in_=q_bf[:, rows, :].rearrange("p n j -> p (n j)"),
             )
 
         k_codes = []
         for first in range(0, N, P):
-            codes = reuse.tile([P, P], U32, name="k_codes%d" % first, offset=4 * (T + N - P - first), align_bytes=64)
+            codes = reuse.tile([P, P], U32, name="k_codes%d" % first, offset=4 * (N - P - first), align_bytes=64)
             nc.vector.tensor_copy(
                 codes[:], word_pool[:].bitcast(U32).indirect(offsets[:, first // 16 : (first + P) // 16])
             )

@@ -49,9 +49,9 @@ def tile_attend_cosexp_topk_kernel(tc, qT, k_words, k_scales, rk, rq, offs, out)
         word_pool = keep.tile([P, T], I32, name="word_pool", align_bytes=64)
         nc.sync.dma_start(word_pool[:], k_words[0].rearrange("p t r -> p (t r)").bitcast(I32))
 
-        zero = reuse.tile([P, 1], F32, name="zero", offset=FIRST, align_bytes=64)
+        zero = keep.tile([P, 1], F32, name="zero")
         nc.vector.memset(zero[:], 0.0)
-        square_zero = reuse.tile([P, P], F32, name="square_zero", offset=FIRST + 64, align_bytes=64)
+        square_zero = reuse.tile([P, P], F32, name="square_zero", offset=FIRST, align_bytes=64)
         nc.vector.memset(square_zero[:], 0.0)
         ident = keep.tile([P, P], F32, name="ident")
         nc.gpsimd.affine_select(
@@ -72,9 +72,6 @@ def tile_attend_cosexp_topk_kernel(tc, qT, k_words, k_scales, rk, rq, offs, out)
         ten = reuse.tile([P, 1], F32, name="ten", offset=0, align_bytes=64)
         nc.scalar.activation(ten[:], zero[:], COPY, bias=10.0)
 
-        k_scale = reuse.tile([P, N // 4], I32, name="k_scale", offset=FIRST, align_bytes=64)
-        nc.gpsimd.memset(k_scale[:], 0)
-
         pieces = ((0, NH), (NH, NH + P), (NH + P, N))
         rk_col = keep.tile([P, N // P], F32, name="rk_col")
         rk_all = keep.tile([P, N], F32, name="rk_all")
@@ -86,10 +83,11 @@ def tile_attend_cosexp_topk_kernel(tc, qT, k_words, k_scales, rk, rq, offs, out)
 
         picked_scales = keep.tile([P, N], U8, name="picked_scales", align_bytes=64)
         nc.vector.tensor_copy(picked_scales[:], scale_pool[:].bitcast(U8).indirect(offsets[:]))
+        k_scale = reuse.tile([P, N // 4], I32, name="k_scale", offset=FIRST, align_bytes=64)
         for quad in range(4):
             first = SCALE_PART + 4 * quad
             queue = (nc.scalar, nc.sync)[quad % 2]
-            queue.dma_start(k_scale[32 * quad : 32 * quad + 4, :], picked_scales[first : first + 4, :].bitcast(I32))
+            queue.dma_start(k_scale[32 * quad : 32 * quad + 32, :], picked_scales[first : first + 32, :].bitcast(I32))
 
         for piece, (first, last) in enumerate(pieces):
             blocks = range(first // P, last // P)

from contextlib import ExitStack

import concourse.mybir as mybir

D, NQ, N, T = 512, 256, 512, 2048
FLOPS = 2 * D * NQ * N

F32 = mybir.dt.float32
BF16 = mybir.dt.bfloat16
I32 = mybir.dt.int32
U32 = mybir.dt.uint32
U16 = mybir.dt.uint16
U8 = mybir.dt.uint8
FP8X4 = mybir.dt.float8_e4m3fn_x4
EXP = mybir.ActivationFunctionType.Exp
COPY = mybir.ActivationFunctionType.Copy
MULT = mybir.AluOpType.mult
NOT_EQUAL = mybir.AluOpType.not_equal

P = 128
PACK = 4
QT = NQ // P
HALVES = 2
NH = N // HALVES
BLOCKS = NH // P
RK_PART = P - 1
SCALE_ROWS = D // 32
SCALE_PART = 64 - SCALE_ROWS
BANK = 2048
FIRST = 4 * N
SECOND = FIRST + 1024


def tile_attend_cosexp_topk_kernel(tc, qT, k_words, k_scales, rk, rq, offs, out):
    nc = tc.nc
    with ExitStack() as ctx:
        keep = ctx.enter_context(tc.tile_pool(name="keep", bufs=1))
        reuse = ctx.enter_context(tc.tile_pool(name="reuse", bufs=1))
        psum = ctx.enter_context(tc.psum_pool(name="psum", bufs=1))

        offsets = keep.tile([P, N // 16], U16, name="offsets")
        nc.sync.dma_start(offsets[:], offs)
        rk_pool = keep.tile([P, T], F32, name="rk_pool", align_bytes=64)
        nc.sync.dma_start(rk_pool[RK_PART : RK_PART + 1, :], rk[0:1, :])
        scale_pool = keep.tile([P, T // 4], I32, name="scale_pool", align_bytes=64)
        nc.scalar.dma_start(scale_pool[SCALE_PART:64, :], k_scales[0].bitcast(I32))
        q_raw = keep.tile([P, PACK, NQ], F32, name="q_raw")
        nc.scalar.dma_start(q_raw[:], qT[0].rearrange("(p j) n -> p j n", j=PACK))
        word_pool = keep.tile([P, T], I32, name="word_pool", align_bytes=64)
        nc.sync.dma_start(word_pool[:], k_words[0].rearrange("p t r -> p (t r)").bitcast(I32))

        zero = keep.tile([P, 1], F32, name="zero")
        nc.vector.memset(zero[:], 0.0)
        square_zero = reuse.tile([P, P], F32, name="square_zero", offset=FIRST, align_bytes=64)
        nc.vector.memset(square_zero[:], 0.0)
        ident = keep.tile([P, P], F32, name="ident")
        nc.gpsimd.affine_select(
            out=ident[:],
            in_=square_zero[:],
            pattern=[[-1, P]],
            compare_op=NOT_EQUAL,
            fill=1.0,
            base=0,
            channel_multiplier=1,
        )
        nc.vector.memset(rk_pool[:RK_PART, :], 0.0)
        nc.vector.memset(scale_pool[:SCALE_PART, :], 0)
        nc.vector.memset(scale_pool[64:, :], 0)

        minus_ten = keep.tile([P, 1], F32, name="minus_ten")
        nc.scalar.activation(minus_ten[:], zero[:], COPY, bias=-10.0)
        ten = reuse.tile([P, 1], F32, name="ten", offset=0, align_bytes=64)
        nc.scalar.activation(ten[:], zero[:], COPY, bias=10.0)

        pieces = ((0, NH), (NH, NH + P), (NH + P, N))
        rk_col = keep.tile([P, N // P], F32, name="rk_col")
        rk_all = keep.tile([P, N], F32, name="rk_all")
        rk_rows = []
        for first, last in pieces:
            rk_row = reuse.tile([P, last - first], F32, name="rk_row%d" % first, offset=SECOND + 4 * first, align_bytes=64)
            nc.scalar.activation(rk_row[:], rk_pool[:].indirect(offsets[:, first // 16 : last // 16]), COPY)
            rk_rows.extend(rk_row[:, c : c + P] for c in range(0, last - first, P))

        picked_scales = keep.tile([P, N], U8, name="picked_scales", align_bytes=64)
        nc.vector.tensor_copy(picked_scales[:], scale_pool[:].bitcast(U8).indirect(offsets[:]))
        k_scale = reuse.tile([P, N // 4], I32, name="k_scale", offset=FIRST, align_bytes=64)
        for quad in range(4):
            first = SCALE_PART + 4 * quad
            queue = (nc.scalar, nc.sync)[quad % 2]
            queue.dma_start(k_scale[32 * quad : 32 * quad + 32, :], picked_scales[first : first + 32, :].bitcast(I32))

        for piece, (first, last) in enumerate(pieces):
            blocks = range(first // P, last // P)
            turned = psum.tile([P, len(blocks), P], F32, name="turned%d" % piece, offset=BANK * (5 + piece))
            for b, block in enumerate(blocks):
                nc.tensor.transpose(turned[:, b, :], rk_rows[block], ident[:])
            nc.scalar.copy(rk_col[:, blocks.start : blocks.stop], turned[:, :, RK_PART])

        rq_sb = reuse.tile([P, QT], F32, name="rq_sb", offset=SECOND, align_bytes=64)
        with nc.allow_non_contiguous_dma(reason="one factor a partition"):
            nc.sync.dma_start(rq_sb[:], rq[0].rearrange("(m p) o -> p (m o)", m=QT))

        for block in range(N // P):
            spread = psum.tile([P, P], F32, name="spread%d" % block, offset=BANK * (4 + block))
            nc.tensor.transpose(spread[:], rk_col[:, block : block + 1].to_broadcast([P, P]), ident[:])
            nc.scalar.activation(
                rk_all[:, block * P : (block + 1) * P], spread[:], COPY, scale=ten[:] if block < BLOCKS else 10.0
            )

        q_codes = keep.tile([P, NQ], U32, name="q_codes", align_bytes=64)
        q_scale = keep.tile([P, NQ], U8, name="q_scale", align_bytes=64)
        q_bf = keep.tile([P, NQ, PACK], BF16, name="q_bf", align_bytes=64)
        for m in range(QT):
            rows = slice(m * P, (m + 1) * P)
            nc.vector.tensor_copy(
                q_bf[:, rows, :].rearrange("p (c i) j -> p c j i", i=4),
                q_raw[:, :, rows].rearrange("p j (c i) -> p c j i", i=4),
            )
        for m in range(QT):
            rows = slice(m * P, (m + 1) * P)
            nc.vector.quantize_mx(
                out=q_codes[:, rows].bitcast(FP8X4),
                scales=q_scale[:, rows],
                in_=q_bf[:, rows, :].rearrange("p n j -> p (n j)"),
            )

        k_codes = []
        for first in range(0, N, P):
            codes = reuse.tile([P, P], U32, name="k_codes%d" % first, offset=4 * (N - P - first), align_bytes=64)
            nc.vector.tensor_copy(
                codes[:], word_pool[:].bitcast(U32).indirect(offsets[:, first // 16 : (first + P) // 16])
            )
            k_codes.append(codes)

        out_by_tile = out[0].rearrange("(m p) n -> p m n", m=QT)
        for block in range(N // P):
            slots = slice(block * P, (block + 1) * P)
            res = keep.tile([P, QT, P], F32, name="res%d" % block)
            for m in range(QT):
                rows = slice(m * P, (m + 1) * P)
                step = block * QT + m
                acc = psum.tile([P, P], F32, name="acc%d" % step, offset=BANK * (block, 4 + (0, 2, 3, 1)[block])[m])
                nc.tensor.matmul_mx(
                    out=acc[:],
                    lhsT=q_codes[:, rows].bitcast(FP8X4),
                    lhsT_scale=q_scale[:, rows],
                    rhs=k_codes[block][:].bitcast(FP8X4),
                    rhs_scale=k_scale[:].bitcast(U8)[:, slots],
                    start=True,
                    stop=True,
                )
                scaled = keep.tile([P, P], F32, name="scaled%d" % step)
                nc.vector.tensor_tensor(scaled[:], acc[:], rk_all[:, slots], MULT)
                nc.scalar.activation(res[:, m, :], scaled[:], EXP, bias=minus_ten[:], scale=rq_sb[:, m : m + 1])
                if block == 0:
                    nc.sync.dma_start(out_by_tile[:, m, slots], res[:, m, :])
            if block > 0:
                nc.sync.dma_start(out_by_tile[:, :, slots], res[:])
